import numpy as np
import ml_dtypes


def mxq(x, axis, fmt="e4m3"):
    dtype, down = {"e4m3": (ml_dtypes.float8_e4m3fn, 7), "e5m2": (ml_dtypes.float8_e5m2, 14)}[fmt]
    v = np.moveaxis(np.asarray(x, np.float32).astype(ml_dtypes.bfloat16).astype(np.float64), axis, -1)
    blocks = v.reshape(v.shape[:-1] + (-1, 32))
    amax = np.abs(blocks).max(-1, keepdims=True)
    byte = np.maximum(np.where(amax > 0, np.frexp(amax)[1] - 1 + 127, 0) - down, 1)
    scale = np.exp2(byte - 127.0)
    codes = (blocks / scale).astype(np.float32).astype(dtype).astype(np.float64)
    return np.moveaxis((codes * scale).reshape(v.shape), -1, axis)


WIDE = False


def mx_kscale(k):
    if not WIDE:
        return np.ones(k)
    levels = np.array([10, -10, 5, -5, 0])
    if k % 512:
        return np.exp2(np.random.permutation(np.resize(levels, k // 32))).repeat(32)
    a = np.empty((k // 512, 16))
    for p in range(k // 512):
        a[p, :8] = np.random.permutation(np.resize(levels, 8))
        for g in range(8):
            far = levels[np.abs(levels - a[p, g]) >= 10]
            a[p, g + 8] = far[np.random.randint(len(far))]
    return np.exp2(a.ravel()).repeat(32)


def f64(x):
    return np.asarray(x).astype(np.float64)


def striped(idx):
    return np.tile(idx.reshape(-1, 16).T, (8, 1)).astype(np.uint16)


def unstriped(offs):
    return offs[:16].T.reshape(-1).astype(np.int64)


E2M1 = np.array([0.0, 0.5, 1.0, 1.5, 2.0, 3.0, 4.0, 6.0, -0.0, -0.5, -1.0, -1.5, -2.0, -3.0, -4.0, -6.0])


def pack_weight(w, fmt):
    k, n = w.shape
    w = f64(np.asarray(w, np.float32).astype(ml_dtypes.bfloat16)).reshape(k // 32, 32, n)
    amax = np.abs(w).max(1)
    if fmt == "e4m3":
        byte = np.frexp(amax)[1] - 1 + 127 - 7
    else:
        mant, ex = np.frexp(amax / 6.0)
        byte = np.where(mant > 0.5, ex, ex - 1) + 127
    byte = np.clip(np.where(amax > 0, byte, 1), 1, 254)
    scaled = (w * np.exp2(127.0 - byte)[:, None, :]).reshape(k, n).astype(np.float32)
    by_word = np.ascontiguousarray(scaled.reshape(k // 512, 128, 4, n).transpose(0, 1, 3, 2))
    if fmt == "e4m3":
        words = by_word.astype(ml_dtypes.float8_e4m3fn).view(np.uint8)
    else:
        c = by_word.astype(ml_dtypes.float4_e2m1fn).view(np.uint8) & 0xF
        words = (c[..., 0::2] | (c[..., 1::2] << 4)).reshape(k // 512, 128, 2 * n)
    return np.ascontiguousarray(words), np.ascontiguousarray(byte.astype(np.uint8).reshape(k // 512, 16, n))


def unpack_weight(words, scales, fmt):
    g, _, n = scales.shape
    words = np.ascontiguousarray(words).reshape(g, 128, n, -1)
    if fmt == "e4m3":
        vals = words.view(ml_dtypes.float8_e4m3fn).astype(np.float64)
    else:
        nib = np.empty((g, 128, n, 4), np.uint8)
        nib[..., 0::2] = words & 0xF
        nib[..., 1::2] = words >> 4
        vals = E2M1[nib]
    vals = vals * np.repeat(np.exp2(scales.astype(np.float64) - 127.0), 8, axis=1)[..., None]
    return vals.transpose(0, 1, 3, 2).reshape(g * 512, n)


def gelu(v):
    return 0.5 * v * (1.0 + np.tanh(np.sqrt(2.0 / np.pi) * (v + 0.044715 * v**3)))


def often(T, S):
    return np.random.permutation(T)[(T * np.random.uniform(0, 1, S) ** 4).astype(np.int64)]


def bf(x):
    return np.asarray(x, np.float32).astype(ml_dtypes.bfloat16)


def planes(Y):
    n, m = Y.shape
    b = f64(bf(Y)).reshape(n // 32, 32, m)
    amax = np.abs(b).max(1)
    byte = np.clip(np.where(amax > 0, np.frexp(amax)[1] - 1 + 127 - 7, 1), 1, 254)
    codes = (b * np.exp2(127.0 - byte)[:, None, :]).reshape(n, m).astype(np.float32).astype(ml_dtypes.float8_e4m3fn).view(np.uint8)
    words = codes.reshape(n // 512, 128, 4, m).transpose(0, 1, 3, 2)
    return np.ascontiguousarray(words), np.ascontiguousarray(byte.astype(np.uint8).reshape(n // 512, 16, m))


K, T, S, P, H, N = 1024, 2048, 1024, 512, 512, 1024


def setup_inputs():
    n = np.random.standard_normal
    s = mx_kscale(K)[:, None]
    u = mx_kscale(H)[:, None]
    inp = {}
    inp["tab_words"], inp["tab_scales"] = pack_weight(n((K, T)) * s, "e4m3")
    inp["tab2_words"], inp["tab2_scales"] = pack_weight(n((K, T)) * s, "e4m3")
    inp["tab3_words"], inp["tab3_scales"] = pack_weight(n((K, T)) * s, "e4m3")
    inp["offs"] = striped(np.random.permutation(T)[:S])
    inp["offs2"] = striped(np.random.permutation(T)[:S])
    inp["offs3"] = striped(np.random.permutation(T)[:S])
    inp["pos1"] = striped(np.random.permutation(S)[:P])
    inp["pos2"] = striped(often(S, P))
    inp["pos3"] = striped(often(S, P))
    inp["wa"] = (n((K, H)) / K**0.5 / s * u.T).astype(np.float32)
    inp["w4_words"], inp["w4_scales"] = pack_weight(n((K, H)) / K**0.5 / s * u.T, "e2m1")
    inp["w8_words"], inp["w8_scales"] = pack_weight(n((K, H)) / K**0.5 / s * u.T, "e4m3")
    inp["sp"] = (n((H, P)) * u).astype(np.float32)
    inp["wo"] = (n((H, N)) / H**0.5 / u * np.exp(0.8 * n(N))).astype(np.float32)
    return inp


def reference(tab_words, tab_scales, tab2_words, tab2_scales, tab3_words, tab3_scales, offs, offs2, offs3,
              pos1, pos2, pos3, wa, w4_words, w4_scales, w8_words, w8_scales, sp, wo):
    v = unpack_weight(tab_words, tab_scales, "e4m3")[:, unstriped(offs)]
    v2 = unpack_weight(tab2_words, tab2_scales, "e4m3")[:, unstriped(offs2)]
    v3 = unpack_weight(tab3_words, tab3_scales, "e4m3")[:, unstriped(offs3)]
    a = mxq(f64(wa), 0, "e4m3").T @ v
    b = unpack_weight(w4_words, w4_scales, "e2m1").T @ v2
    d = unpack_weight(w8_words, w8_scales, "e4m3").T @ v3
    sp64 = f64(sp)
    over = np.maximum(a[:, unstriped(pos1)], sp64)
    under = np.minimum(b[:, unstriped(pos2)], sp64)
    z = over - under + d[:, unstriped(pos3)]
    y = mxq(f64(wo), 0, "e4m3").T @ mxq(z, 0, "e4m3")
    words, scales = planes(y)
    return y, words, scales

@@ -1,0 +1,339 @@
+from contextlib import ExitStack
+
+import concourse.mybir as mybir
+
+K, T, S, J, H, N = 1024, 2048, 1024, 512, 512, 1024
+FLOPS = 2 * (3 * K * H * S + H * N * J)
+
+F32 = mybir.dt.float32
+BF16 = mybir.dt.bfloat16
+I32 = mybir.dt.int32
+U32 = mybir.dt.uint32
+U16 = mybir.dt.uint16
+U8 = mybir.dt.uint8
+FP8X4 = mybir.dt.float8_e4m3fn_x4
+FP4X4 = mybir.dt.float4_e2m1fn_x4
+ALU = mybir.AluOpType
+ACT = mybir.ActivationFunctionType
+
+P = 128
+PACK = 4
+PASSES = K // (P * PACK)
+QUADS = 4
+BANK = 512
+HALVES = S // BANK
+GROUPS = N // (P * PACK)
+RUN = 8
+CHUNK = 256
+BLOCK = 128
+
+
+def tile_list_air_network_join_kernel(
+    tc, tab_words, tab_scales, tab2_words, tab2_scales, tab3_words, tab3_scales,
+    offs, offs2, offs3, pos1, pos2, pos3, wa, w4_words, w4_scales, w8_words, w8_scales, sp, wo,
+    out_0, out_1, out_2,
+):
+    nc = tc.nc
+    with ExitStack() as ctx:
+        held = ctx.enter_context(tc.tile_pool(name="held", bufs=1))
+        ring = ctx.enter_context(tc.tile_pool(name="ring", bufs=1))
+        psum = ctx.enter_context(tc.psum_pool(name="psum", bufs=8))
+
+        def load_list(name, src):
+            lst = held.tile(list(src.shape), U16, name=name)
+            nc.sync.dma_start(lst[:], src)
+            return lst
+
+        def zeroed_plane(name, shape):
+            plane = held.tile(shape, U8, name=name, align_bytes=64)
+            nc.vector.memset(plane[:].bitcast(I32), 0)
+            return plane
+
+        def load_packed_scales(plane, src):
+            for q in range(QUADS):
+                nc.sync.dma_start(
+                    plane[32 * q : 32 * q + 4 * PASSES, :].bitcast(I32),
+                    src[:, 4 * q : 4 * q + 4, :].bitcast(I32),
+                )
+
+        def load_table_pass(name, words, a, tag="window", bufs=3):
+            win = ring.tile([P, T], I32, name=name, tag=tag, bufs=bufs, align_bytes=64)
+            nc.sync.dma_start(win[:], words[a].rearrange("p c i -> p (c i)").bitcast(I32))
+            return win
+
+        def raw_tile(name):
+            return ring.tile([P, PACK, 512], F32, name=name, tag="raw", bufs=2, align_bytes=64)
+
+        def load_wa(a):
+            raw = raw_tile("wa_raw%d" % a)
+            nc.sync.dma_start(raw[:], wa[512 * a : 512 * (a + 1), :].rearrange("(p i) c -> p i c", i=PACK))
+            return raw
+
+        def load_dealt_rows(dst, src):
+            rows = src.rearrange("(b t i) c -> t b i c", t=PACK, i=RUN)
+            for t in range(PACK):
+                nc.sync.dma_start(dst[:, t, :], rows[t])
+
+        def load_wo(g):
+            raw = raw_tile("wo_raw%d" % g)
+            load_dealt_rows(raw, wo[:, 512 * g : 512 * (g + 1)])
+            return raw
+
+        sb_win = zeroed_plane("sb_win", [P, T])
+        w4s_raw = zeroed_plane("w4s_raw", [P, PASSES, H])
+        sa_win = zeroed_plane("sa_win", [P, T])
+        w8s_raw = zeroed_plane("w8s_raw", [P, H])
+        sd_win = zeroed_plane("sd_win", [P, T])
+        sb_second = zeroed_plane("sb_second", [P, S])
+
+        list_b = load_list("list_b", offs2)
+        tb0 = load_table_pass("tb0", tab2_words, 0)
+        wa_raw0 = load_wa(0)
+        load_packed_scales(sb_win, tab2_scales)
+        tb1 = load_table_pass("tb1", tab2_words, 1)
+        wa_raw1 = load_wa(1)
+        w4_raw = held.tile([P, PASSES, 2 * H], U8, name="w4_raw", align_bytes=64)
+        nc.sync.dma_start(w4_raw[:].bitcast(I32), w4_words.rearrange("a p c -> p a c").bitcast(I32))
+        for q in range(QUADS):
+            nc.sync.dma_start(
+                w4s_raw[32 * q : 32 * q + 4, :, :].bitcast(I32),
+                w4_scales[:, 4 * q : 4 * q + 4, :].rearrange("a r c -> r a c").bitcast(I32),
+            )
+        list_a = load_list("list_a", offs)
+        ta0 = load_table_pass("ta0", tab_words, 0)
+        load_packed_scales(sa_win, tab_scales)
+        ta1 = load_table_pass("ta1", tab_words, 1)
+        load_packed_scales(w8s_raw, w8_scales)
+        w8_raw = held.tile([P, PASSES, H], I32, name="w8_raw", align_bytes=64)
+        nc.sync.dma_start(w8_raw[:], w8_words.rearrange("a p c i -> p a (c i)").bitcast(I32))
+        list_d = load_list("list_d", offs3)
+        td0 = load_table_pass("td0", tab3_words, 0)
+        load_packed_scales(sd_win, tab3_scales)
+        wo_raw0 = load_wo(0)
+        pick_b = load_list("pick_b", pos2)
+        td1 = load_table_pass("td1", tab3_words, 1, tag="last_window", bufs=1)
+        pick_a = load_list("pick_a", pos1)
+        pick_d = load_list("pick_d", pos3)
+        sp_sb = held.tile([P, PACK, J], F32, name="sp_sb", align_bytes=64)
+        load_dealt_rows(sp_sb, sp)
+        wo_raw1 = load_wo(1)
+
+        def gather_scales(name, win, lst):
+            got = held.tile([P, S], U8, name=name, align_bytes=64)
+            nc.vector.tensor_copy(got[:], win[:].indirect(lst[:]))
+            return got
+
+        def gather_words(name, win, lst, pieces):
+            got = held.tile([P, S], U32, name=name, align_bytes=64)
+            n = S // pieces
+            for h in range(pieces):
+                nc.vector.tensor_copy(
+                    got[:, n * h : n * (h + 1)],
+                    win[:].bitcast(U32).indirect(lst[:, n // 16 * h : n // 16 * (h + 1)]),
+                )
+            return got
+
+        def deal_words(name, raw, shape, dtype):
+            dealt = held.tile(shape, dtype, name=name, align_bytes=64)
+            src = raw.bitcast(I32)
+            dst = dealt[:].bitcast(I32)
+            if len(shape) == 3:
+                nc.vector.tensor_copy(
+                    dst.rearrange("p a (t b i) -> p a t b i", t=PACK, b=16),
+                    src.rearrange("p a (b t i) -> p a t b i", t=PACK, b=16),
+                )
+            else:
+                nc.vector.tensor_copy(
+                    dst.rearrange("p (t b i) -> p t b i", t=PACK, b=16),
+                    src.rearrange("p (b t i) -> p t b i", t=PACK, b=16),
+                )
+            return dealt
+
+        def rounded_tile(name):
+            return ring.tile([P, 512 * PACK], BF16, name=name, tag="rounded", bufs=2, align_bytes=64)
+
+        def quantize(name, rounded):
+            codes = held.tile([P, 512], U32, name=name + "_codes", align_bytes=64)
+            scales = held.tile([P, 512], U8, name=name + "_scales", align_bytes=64)
+            nc.vector.quantize_mx(out=codes[:].bitcast(FP8X4), scales=scales[:], in_=rounded[:])
+            return codes, scales
+
+        def round_wa(a, raw):
+            rounded = rounded_tile("wa_bf%d" % a)
+            nc.scalar.copy(
+                rounded[:].rearrange("p (t b i j) -> p t b i j", t=PACK, i=RUN, j=PACK),
+                raw[:].rearrange("p j (b t i) -> p t b i j", t=PACK, i=RUN),
+            )
+            return rounded
+
+        def round_wo(g, raw):
+            rounded = rounded_tile("wo_bf%d" % g)
+            nc.scalar.copy(
+                rounded[:].rearrange("p (t m j) -> p m t j", t=PACK, j=PACK),
+                raw[:].rearrange("p j (m t) -> p m t j", t=PACK),
+            )
+            return rounded
+
+        def result_rows(name):
+            return [held.tile([P, S], F32, name="%s_rows%d" % (name, t), align_bytes=64) for t in range(PACK)]
+
+        def first_stage(rows, halves, weights, columns):
+            for h in halves:
+                cols = slice(BANK * h, BANK * (h + 1))
+                for t in range(PACK):
+                    acc = psum.tile([P, BANK], F32, name="acc", tag="bank")
+                    for a in range(PASSES):
+                        w_codes, w_scales = weights(a, t)
+                        c_codes, c_scales = columns(a, cols)
+                        nc.tensor.matmul_mx(
+                            out=acc[:], lhsT=w_codes, lhsT_scale=w_scales, rhs=c_codes, rhs_scale=c_scales,
+                            start=(a == 0), stop=(a == PASSES - 1),
+                        )
+                    nc.scalar.activation(rows[t][:, cols], acc[:], ACT.Copy)
+
+        def slice_cols(t):
+            return slice(P * t, P * (t + 1))
+
+        wa_bf0 = round_wa(0, wa_raw0)
+        vb0 = gather_words("vb0", tb0, list_b, 1)
+        sb = gather_scales("sb", sb_win, list_b)
+        nc.scalar.dma_start(sb_second[0:112, :].bitcast(I32), sb[4:116, :].bitcast(I32))
+        wa_bf1 = round_wa(1, wa_raw1)
+        vb1 = gather_words("vb1", tb1, list_b, HALVES)
+        w4 = deal_words("w4", w4_raw[:], [P, PASSES, 2 * H], U8)
+        w4s = deal_words("w4s", w4s_raw[:], [P, PASSES, H], U8)
+        wa_q = [quantize("wa0", wa_bf0), quantize("wa1", wa_bf1)]
+        b_rows = result_rows("b")
+        first_stage(
+            b_rows, range(HALVES),
+            lambda a, t: (w4[:, a, 2 * P * t : 2 * P * (t + 1)].bitcast(FP4X4), w4s[:, a, slice_cols(t)]),
+            lambda a, cols: ((vb0, vb1)[a][:, cols].bitcast(FP8X4), (sb, sb_second)[a][:, cols]),
+        )
+
+        va0 = gather_words("va0", ta0, list_a, 1)
+        sa = gather_scales("sa", sa_win, list_a)
+        va1 = gather_words("va1", ta1, list_a, HALVES)
+        a_rows = result_rows("a")
+        first_stage(
+            a_rows, range(HALVES),
+            lambda a, t: (wa_q[a][0][:, slice_cols(t)].bitcast(FP8X4), wa_q[a][1][:, slice_cols(t)]),
+            lambda a, cols: ((va0, va1)[a][:, cols].bitcast(FP8X4), sa[4 * a : P, cols]),
+        )
+
+        w8 = deal_words("w8", w8_raw[:], [P, PASSES, H], U32)
+        w8s = deal_words("w8s", w8s_raw[:], [P, H], U8)
+        vd0 = gather_words("vd0", td0, list_d, 1)
+        sd = gather_scales("sd", sd_win, list_d)
+        wo_bf0 = round_wo(0, wo_raw0)
+        vd1 = gather_words("vd1", td1, list_d, HALVES)
+        d_rows = result_rows("d")
+
+        def d_half(h):
+            first_stage(
+                d_rows, [h],
+                lambda a, t: (w8[:, a, slice_cols(t)].bitcast(FP8X4), w8s[4 * a : P, slice_cols(t)]),
+                lambda a, cols: ((vd0, vd1)[a][:, cols].bitcast(FP8X4), sd[4 * a : P, cols]),
+            )
+
+        wo_codes = ring.tile([P, GROUPS, 512], U32, name="wo_codes", tag="last_window", bufs=1, align_bytes=64)
+        wo_scales = held.tile([P, GROUPS, 512], U8, name="wo_scales", align_bytes=64)
+
+        def quantize_wo(g, rounded):
+            nc.vector.quantize_mx(out=wo_codes[:, g, :].bitcast(FP8X4), scales=wo_scales[:, g, :], in_=rounded[:])
+
+        y_codes = held.tile([P, GROUPS, J], U32, name="y_codes", align_bytes=64)
+        y_scales = held.tile([P, GROUPS, J], U8, name="y_scales", align_bytes=64)
+        out_rows = out_0.rearrange("(g p t) j -> g p t j", p=P, t=PACK)
+        out_words = out_1.rearrange("g p m t -> p g (m t)").bitcast(I32)
+
+        def picks(lst, start, count):
+            return lst[:, start // 16 : (start + count) // 16]
+
+        def shortfall(c0, tag):
+            below = ring.tile([P, PACK, CHUNK], F32, name="below", tag=tag, bufs=1, align_bytes=64)
+            short = ring.tile([P, PACK, CHUNK], F32, name="short", tag="short", bufs=1, align_bytes=64)
+            for t in range(PACK):
+                nc.vector.tensor_tensor(
+                    below[:, t, :], b_rows[t][:].indirect(picks(pick_b, c0, CHUNK)), sp_sb[:, t, c0 : c0 + CHUNK], ALU.subtract
+                )
+            nc.scalar.activation(short[:], below[:], ACT.Relu, scale=-1.0)
+            return short
+
+        def spread(c0, short, tag):
+            above = ring.tile([P, PACK, CHUNK], F32, name="above", tag=tag, bufs=1, align_bytes=64)
+            for t in range(PACK):
+                nc.vector.tensor_tensor(
+                    above[:, t, :], a_rows[t][:].indirect(picks(pick_a, c0, CHUNK)), sp_sb[:, t, c0 : c0 + CHUNK], ALU.subtract
+                )
+            nc.vector.scalar_tensor_tensor(above[:], above[:], 0.0, short[:], ALU.max, ALU.add)
+            return above
+
+        def joined(j0, width, above, tag):
+            inside = j0 % CHUNK
+            z = ring.tile([P, PACK, width], F32, name="z", tag="z", bufs=2, align_bytes=64)
+            for t in range(PACK):
+                nc.vector.tensor_tensor(
+                    z[:, t, :], d_rows[t][:].indirect(picks(pick_d, j0, width)),
+                    above[:, t, inside : inside + width], ALU.add,
+                )
+            z_bf = ring.tile([P, width * PACK], BF16, name="z_bf", tag=tag, bufs=1, align_bytes=64)
+            nc.scalar.copy(
+                z_bf[:].rearrange("p (c i t) -> p c t i", i=4, t=PACK),
+                z[:].rearrange("p t (c i) -> p c t i", i=4),
+            )
+            z_codes = ring.tile([P, width], U32, name="z_codes", tag="z_codes", bufs=4, align_bytes=64)
+            z_scales = ring.tile([P, width], U8, name="z_scales", tag="z_scales", bufs=4, align_bytes=64)
+            nc.vector.quantize_mx(out=z_codes[:].bitcast(FP8X4), scales=z_scales[:], in_=z_bf[:])
+            return z_codes, z_scales
+
+        def second_stage(j0, width, z_q, round_on_vector):
+            cols = slice(j0, j0 + width)
+            for g in range(GROUPS):
+                y = ring.tile([P, PACK, width], F32, name="y", tag="y", bufs=4, align_bytes=64)
+                y_bf = ring.tile([P, width, PACK], BF16, name="y_bf", tag="y_bf", bufs=4, align_bytes=64)
+                for k in range(width // BLOCK):
+                    block = slice(BLOCK * k, BLOCK * (k + 1))
+                    acc = psum.tile([P, PACK, BLOCK], F32, name="y_acc", tag="bank")
+                    for t in range(PACK):
+                        nc.tensor.matmul_mx(
+                            out=acc[:, t, :], lhsT=wo_codes[:, g, slice_cols(t)].bitcast(FP8X4),
+                            lhsT_scale=wo_scales[:, g, slice_cols(t)], rhs=z_q[0][:, block].bitcast(FP8X4),
+                            rhs_scale=z_q[1][:, block], start=True, stop=True,
+                        )
+                    turned = acc[:].rearrange("p t j -> p j t")
+                    if not round_on_vector:
+                        nc.scalar.copy(y[:, :, block], acc[:])
+                        nc.scalar.copy(y_bf[:, block, :], turned)
+                    elif g == 0:
+                        nc.scalar.copy(y[:, :, block], acc[:])
+                        nc.vector.tensor_copy(y_bf[:, block, :], turned)
+                    else:
+                        nc.vector.tensor_copy(y_bf[:, block, :], turned)
+                        nc.scalar.copy(y[:, :, block], acc[:])
+                nc.sync.dma_start(out_rows[g][:, :, cols], y[:])
+                nc.vector.quantize_mx(
+                    out=y_codes[:, g, cols].bitcast(FP8X4), scales=y_scales[:, g, cols],
+                    in_=y_bf[:].rearrange("p j t -> p (j t)"),
+                )
+            nc.sync.dma_start(out_words[:, :, cols], y_codes[:, :, cols].bitcast(I32))
+
+        d_half(0)
+        quantize_wo(0, wo_bf0)
+        short = shortfall(0, "below0")
+        d_half(1)
+        above = spread(0, short, "above0")
+        quantize_wo(1, round_wo(1, wo_raw1))
+        z_q = [joined(0, BLOCK, above, "above1"), joined(BLOCK, BLOCK, above, "below1")]
+        second_stage(0, BLOCK, z_q[0], False)
+        short = shortfall(CHUNK, "below1")
+        second_stage(BLOCK, BLOCK, z_q[1], False)
+        above = spread(CHUNK, short, "above1")
+        z_q = [joined(CHUNK, BLOCK, above, "below0"), joined(CHUNK + BLOCK, BLOCK, above, "above0")]
+        second_stage(CHUNK, BLOCK, z_q[0], True)
+        second_stage(CHUNK + BLOCK, BLOCK, z_q[1], True)
+
+        for q in range(QUADS):
+            nc.sync.dma_start(
+                out_2[:, 4 * q : 4 * q + 4, :].rearrange("g r m -> r g m").bitcast(I32),
+                y_scales[32 * q : 32 * q + 4, :, :].bitcast(I32),
+            )

@@ -37,27 +37,27 @@ def tile_list_air_network_join_kernel(
     with ExitStack() as ctx:
         held = ctx.enter_context(tc.tile_pool(name="held", bufs=1))
         ring = ctx.enter_context(tc.tile_pool(name="ring", bufs=1))
-        psum = ctx.enter_context(tc.psum_pool(name="psum", bufs=8))
+        psum = ctx.enter_context(tc.psum_pool(name="psum", bufs=4))
 
         def load_list(name, src):
             lst = held.tile(list(src.shape), U16, name=name)
             nc.sync.dma_start(lst[:], src)
             return lst
 
-        def zeroed_plane(name, shape):
-            plane = held.tile(shape, U8, name=name, align_bytes=64)
+        def zeroed_plane(name, width, tag=None):
+            plane = held.tile([P, width + 4], U8, name=name, tag=tag or name, align_bytes=64)
             nc.vector.memset(plane[:].bitcast(I32), 0)
-            return plane
+            return plane[:, 0:width]
 
-        def load_packed_scales(plane, src):
+        def load_packed_scales(plane, src, queue=nc.sync):
             for q in range(QUADS):
-                nc.sync.dma_start(
+                queue.dma_start(
                     plane[32 * q : 32 * q + 4 * PASSES, :].bitcast(I32),
                     src[:, 4 * q : 4 * q + 4, :].bitcast(I32),
                 )
 
-        def load_table_pass(name, words, a, tag="window", bufs=3):
-            win = ring.tile([P, T], I32, name=name, tag=tag, bufs=bufs, align_bytes=64)
+        def load_table_pass(name, words, a, tag):
+            win = held.tile([P, T], I32, name=name, tag=tag, align_bytes=64)
             nc.sync.dma_start(win[:], words[a].rearrange("p c i -> p (c i)").bitcast(I32))
             return win
 
@@ -74,23 +74,24 @@ def tile_list_air_network_join_kernel(
             for t in range(PACK):
                 nc.sync.dma_start(dst[:, t, :], rows[t])
 
-        def load_wo(g):
-            raw = raw_tile("wo_raw%d" % g)
+        def load_wo(g, tag=None):
+            raw = held.tile([P, PACK, 512], F32, name="wo_raw", tag=tag, align_bytes=64) if tag else raw_tile("wo_raw%d" % g)
             load_dealt_rows(raw, wo[:, 512 * g : 512 * (g + 1)])
             return raw
 
-        sb_win = zeroed_plane("sb_win", [P, T])
-        w4s_raw = zeroed_plane("w4s_raw", [P, PASSES, H])
-        sa_win = zeroed_plane("sa_win", [P, T])
-        w8s_raw = zeroed_plane("w8s_raw", [P, H])
-        sd_win = zeroed_plane("sd_win", [P, T])
-        sb_second = zeroed_plane("sb_second", [P, S])
+        sb_win = zeroed_plane("sb_win", T)
+        sa_win = zeroed_plane("sa_win", T, "wa1_codes")
+        w4s_raw = zeroed_plane("w4s_raw", PASSES * H).rearrange("p (a c) -> p a c", a=PASSES)
+        sb_second = zeroed_plane("sb_second", S)
+        sd_win = zeroed_plane("sd_win", T)
+        w8s_raw = zeroed_plane("w8s_raw", H)
 
         list_b = load_list("list_b", offs2)
-        tb0 = load_table_pass("tb0", tab2_words, 0)
+        tb0 = load_table_pass("tb0", tab2_words, 0, "sb")
+        load_packed_scales(sb_win, tab2_scales, nc.gpsimd)
+        tb1 = load_table_pass("tb1", tab2_words, 1, "wa0_codes")
+        list_a = load_list("list_a", offs)
         wa_raw0 = load_wa(0)
-        load_packed_scales(sb_win, tab2_scales)
-        tb1 = load_table_pass("tb1", tab2_words, 1)
         wa_raw1 = load_wa(1)
         w4_raw = held.tile([P, PASSES, 2 * H], U8, name="w4_raw", align_bytes=64)
         nc.sync.dma_start(w4_raw[:].bitcast(I32), w4_words.rearrange("a p c -> p a c").bitcast(I32))
@@ -99,28 +100,10 @@ def tile_list_air_network_join_kernel(
                 w4s_raw[32 * q : 32 * q + 4, :, :].bitcast(I32),
                 w4_scales[:, 4 * q : 4 * q + 4, :].rearrange("a r c -> r a c").bitcast(I32),
             )
-        list_a = load_list("list_a", offs)
-        ta0 = load_table_pass("ta0", tab_words, 0)
-        load_packed_scales(sa_win, tab_scales)
-        ta1 = load_table_pass("ta1", tab_words, 1)
-        load_packed_scales(w8s_raw, w8_scales)
-        w8_raw = held.tile([P, PASSES, H], I32, name="w8_raw", align_bytes=64)
-        nc.sync.dma_start(w8_raw[:], w8_words.rearrange("a p c i -> p a (c i)").bitcast(I32))
-        list_d = load_list("list_d", offs3)
-        td0 = load_table_pass("td0", tab3_words, 0)
-        load_packed_scales(sd_win, tab3_scales)
-        wo_raw0 = load_wo(0)
-        pick_b = load_list("pick_b", pos2)
-        td1 = load_table_pass("td1", tab3_words, 1, tag="last_window", bufs=1)
-        pick_a = load_list("pick_a", pos1)
-        pick_d = load_list("pick_d", pos3)
-        sp_sb = held.tile([P, PACK, J], F32, name="sp_sb", align_bytes=64)
-        load_dealt_rows(sp_sb, sp)
-        wo_raw1 = load_wo(1)
 
         def gather_scales(name, win, lst):
             got = held.tile([P, S], U8, name=name, align_bytes=64)
-            nc.vector.tensor_copy(got[:], win[:].indirect(lst[:]))
+            nc.vector.tensor_copy(got[:], win.indirect(lst[:]))
             return got
 
         def gather_words(name, win, lst, pieces):
@@ -195,14 +178,34 @@ def tile_list_air_network_join_kernel(
             return slice(P * t, P * (t + 1))
 
         wa_bf0 = round_wa(0, wa_raw0)
+        wa_bf1 = round_wa(1, wa_raw1)
         vb0 = gather_words("vb0", tb0, list_b, 1)
         sb = gather_scales("sb", sb_win, list_b)
-        nc.scalar.dma_start(sb_second[0:112, :].bitcast(I32), sb[4:116, :].bitcast(I32))
-        wa_bf1 = round_wa(1, wa_raw1)
+        load_packed_scales(sa_win, tab_scales)
+        nc.sync.dma_start(sb_second[0:112, :].bitcast(I32), sb[4:116, :].bitcast(I32))
+        ta0 = load_table_pass("ta0", tab_words, 0, "window0")
+        ta1 = load_table_pass("ta1", tab_words, 1, "window2")
+        pick_b = load_list("pick_b", pos2)
+        sp_sb = held.tile([P, PACK, J], F32, name="sp_sb", align_bytes=64)
+        load_dealt_rows(sp_sb, sp)
+        list_d = load_list("list_d", offs3)
+        load_packed_scales(sd_win, tab3_scales)
+        w8_raw = held.tile([P, PASSES, H], I32, name="w8_raw", align_bytes=64)
+        nc.sync.dma_start(w8_raw[:], w8_words.rearrange("a p c i -> p a (c i)").bitcast(I32))
+        load_packed_scales(w8s_raw, w8_scales)
+        pick_a = load_list("pick_a", pos1)
+        wo_raw0 = load_wo(0)
+        td0 = load_table_pass("td0", tab3_words, 0, "window0")
+        wo_raw1 = load_wo(1)
+        td1 = load_table_pass("td1", tab3_words, 1, "wo_codes")
+        pick_d = load_list("pick_d", pos3)
+
         vb1 = gather_words("vb1", tb1, list_b, HALVES)
         w4 = deal_words("w4", w4_raw[:], [P, PASSES, 2 * H], U8)
-        w4s = deal_words("w4s", w4s_raw[:], [P, PASSES, H], U8)
-        wa_q = [quantize("wa0", wa_bf0), quantize("wa1", wa_bf1)]
+        w4s = deal_words("w4s", w4s_raw, [P, PASSES, H], U8)
+        wa_q = [quantize("wa0", wa_bf0)]
+        sa = gather_scales("sa", sa_win, list_a)
+        wa_q.append(quantize("wa1", wa_bf1))
         b_rows = result_rows("b")
         first_stage(
             b_rows, range(HALVES),
@@ -211,7 +214,6 @@ def tile_list_air_network_join_kernel(
         )
 
         va0 = gather_words("va0", ta0, list_a, 1)
-        sa = gather_scales("sa", sa_win, list_a)
         va1 = gather_words("va1", ta1, list_a, HALVES)
         a_rows = result_rows("a")
         first_stage(
@@ -220,12 +222,6 @@ def tile_list_air_network_join_kernel(
             lambda a, cols: ((va0, va1)[a][:, cols].bitcast(FP8X4), sa[4 * a : P, cols]),
         )
 
-        w8 = deal_words("w8", w8_raw[:], [P, PASSES, H], U32)
-        w8s = deal_words("w8s", w8s_raw[:], [P, H], U8)
-        vd0 = gather_words("vd0", td0, list_d, 1)
-        sd = gather_scales("sd", sd_win, list_d)
-        wo_bf0 = round_wo(0, wo_raw0)
-        vd1 = gather_words("vd1", td1, list_d, HALVES)
         d_rows = result_rows("d")
 
         def d_half(h):
@@ -235,7 +231,6 @@ def tile_list_air_network_join_kernel(
                 lambda a, cols: ((vd0, vd1)[a][:, cols].bitcast(FP8X4), sd[4 * a : P, cols]),
             )
 
-        wo_codes = ring.tile([P, GROUPS, 512], U32, name="wo_codes", tag="last_window", bufs=1, align_bytes=64)
         wo_scales = held.tile([P, GROUPS, 512], U8, name="wo_scales", align_bytes=64)
 
         def quantize_wo(g, rounded):
@@ -249,8 +244,8 @@ def tile_list_air_network_join_kernel(
         def picks(lst, start, count):
             return lst[:, start // 16 : (start + count) // 16]
 
-        def shortfall(c0, tag):
-            below = ring.tile([P, PACK, CHUNK], F32, name="below", tag=tag, bufs=1, align_bytes=64)
+        def shortfall(c0, tag, bufs):
+            below = ring.tile([P, PACK, CHUNK], F32, name="below", tag=tag, bufs=bufs, align_bytes=64)
             short = ring.tile([P, PACK, CHUNK], F32, name="short", tag="short", bufs=1, align_bytes=64)
             for t in range(PACK):
                 nc.vector.tensor_tensor(
@@ -268,9 +263,9 @@ def tile_list_air_network_join_kernel(
             nc.vector.scalar_tensor_tensor(above[:], above[:], 0.0, short[:], ALU.max, ALU.add)
             return above
 
-        def joined(j0, width, above, tag):
+        def joined(j0, width, above, z_tag, tag):
             inside = j0 % CHUNK
-            z = ring.tile([P, PACK, width], F32, name="z", tag="z", bufs=2, align_bytes=64)
+            z = ring.tile([P, PACK, width], F32, name="z", tag=z_tag, bufs=1, align_bytes=64)
             for t in range(PACK):
                 nc.vector.tensor_tensor(
                     z[:, t, :], d_rows[t][:].indirect(picks(pick_d, j0, width)),
@@ -293,47 +288,57 @@ def tile_list_air_network_join_kernel(
                 y_bf = ring.tile([P, width, PACK], BF16, name="y_bf", tag="y_bf", bufs=4, align_bytes=64)
                 for k in range(width // BLOCK):
                     block = slice(BLOCK * k, BLOCK * (k + 1))
-                    acc = psum.tile([P, PACK, BLOCK], F32, name="y_acc", tag="bank")
+                    acc = psum.tile([P, PACK, BLOCK], F32, name="y_acc", tag="y_bank")
                     for t in range(PACK):
                         nc.tensor.matmul_mx(
                             out=acc[:, t, :], lhsT=wo_codes[:, g, slice_cols(t)].bitcast(FP8X4),
                             lhsT_scale=wo_scales[:, g, slice_cols(t)], rhs=z_q[0][:, block].bitcast(FP8X4),
                             rhs_scale=z_q[1][:, block], start=True, stop=True,
                         )
-                    turned = acc[:].rearrange("p t j -> p j t")
-                    if not round_on_vector:
-                        nc.scalar.copy(y[:, :, block], acc[:])
-                        nc.scalar.copy(y_bf[:, block, :], turned)
-                    elif g == 0:
-                        nc.scalar.copy(y[:, :, block], acc[:])
-                        nc.vector.tensor_copy(y_bf[:, block, :], turned)
+                    nc.scalar.copy(y[:, :, block], acc[:])
+                    if round_on_vector:
+                        nc.vector.tensor_copy(
+                            y_bf[:, block, :].rearrange("p (c i) t -> p c t i", i=4),
+                            y[:, :, block].rearrange("p t (c i) -> p c t i", i=4),
+                        )
                     else:
-                        nc.vector.tensor_copy(y_bf[:, block, :], turned)
-                        nc.scalar.copy(y[:, :, block], acc[:])
+                        nc.scalar.copy(y_bf[:, block, :], acc[:].rearrange("p t j -> p j t"))
                 nc.sync.dma_start(out_rows[g][:, :, cols], y[:])
                 nc.vector.quantize_mx(
                     out=y_codes[:, g, cols].bitcast(FP8X4), scales=y_scales[:, g, cols],
                     in_=y_bf[:].rearrange("p j t -> p (j t)"),
                 )
+
+        def store_words(c0):
+            cols = slice(c0, c0 + CHUNK)
             nc.sync.dma_start(out_words[:, :, cols], y_codes[:, :, cols].bitcast(I32))
 
-        d_half(0)
-        quantize_wo(0, wo_bf0)
-        short = shortfall(0, "below0")
-        d_half(1)
+        short = shortfall(0, "below0", 1)
+        sd = gather_scales("sd", sd_win, list_d)
+        w8 = deal_words("w8", w8_raw[:], [P, PASSES, H], U32)
+        w8s = deal_words("w8s", w8s_raw, [P, H], U8)
         above = spread(0, short, "above0")
-        quantize_wo(1, round_wo(1, wo_raw1))
-        z_q = [joined(0, BLOCK, above, "above1"), joined(BLOCK, BLOCK, above, "below1")]
+        wo_bf = [round_wo(0, wo_raw0), round_wo(1, wo_raw1)]
+        vd0 = gather_words("vd0", td0, list_d, 1)
+        vd1 = gather_words("vd1", td1, list_d, HALVES)
+        d_half(0)
+        d_half(1)
+        wo_codes = held.tile([P, GROUPS, 512], U32, name="wo_codes", align_bytes=64)
+        quantize_wo(0, wo_bf[0])
+        quantize_wo(1, wo_bf[1])
+        short = shortfall(CHUNK, "rounded", 2)
+        z_q = [joined(0, BLOCK, above, "z0", "above1"), joined(BLOCK, BLOCK, above, "z1", "z_bf1")]
         second_stage(0, BLOCK, z_q[0], False)
-        short = shortfall(CHUNK, "below1")
         second_stage(BLOCK, BLOCK, z_q[1], False)
+        store_words(0)
         above = spread(CHUNK, short, "above1")
-        z_q = [joined(CHUNK, BLOCK, above, "below0"), joined(CHUNK + BLOCK, BLOCK, above, "above0")]
+        z_q = [joined(CHUNK, BLOCK, above, "z0", "z_bf2"), joined(CHUNK + BLOCK, BLOCK, above, "z1", "z_bf1")]
         second_stage(CHUNK, BLOCK, z_q[0], True)
         second_stage(CHUNK + BLOCK, BLOCK, z_q[1], True)
+        store_words(CHUNK)
 
         for q in range(QUADS):
-            nc.sync.dma_start(
+            nc.scalar.dma_start(
                 out_2[:, 4 * q : 4 * q + 4, :].rearrange("g r m -> r g m").bitcast(I32),
                 y_scales[32 * q : 32 * q + 4, :, :].bitcast(I32),
             )

@@ -1,6 +1,7 @@
 from contextlib import ExitStack
 
 import concourse.mybir as mybir
+from concourse.masks import make_identity
 
 K, T, S, J, H, N = 1024, 2048, 1024, 512, 512, 1024
 FLOPS = 2 * (3 * K * H * S + H * N * J)
@@ -45,13 +46,13 @@ def tile_list_air_network_join_kernel(
             return lst
 
         def zeroed_plane(name, width, tag=None):
-            plane = held.tile([P, width + 4], U8, name=name, tag=tag or name, align_bytes=64)
+            plane = held.tile([P, width], U8, name=name, tag=tag or name, align_bytes=64)
             nc.vector.memset(plane[:].bitcast(I32), 0)
-            return plane[:, 0:width]
+            return plane[:]
 
-        def load_packed_scales(plane, src, queue=nc.sync):
+        def load_packed_scales(plane, src):
             for q in range(QUADS):
-                queue.dma_start(
+                nc.sync.dma_start(
                     plane[32 * q : 32 * q + 4 * PASSES, :].bitcast(I32),
                     src[:, 4 * q : 4 * q + 4, :].bitcast(I32),
                 )
@@ -69,17 +70,12 @@ def tile_list_air_network_join_kernel(
             nc.sync.dma_start(raw[:], wa[512 * a : 512 * (a + 1), :].rearrange("(p i) c -> p i c", i=PACK))
             return raw
 
-        def load_dealt_rows(dst, src):
-            rows = src.rearrange("(b t i) c -> t b i c", t=PACK, i=RUN)
-            for t in range(PACK):
-                nc.sync.dma_start(dst[:, t, :], rows[t])
-
         def load_wo(g, tag=None):
             raw = held.tile([P, PACK, 512], F32, name="wo_raw", tag=tag, align_bytes=64) if tag else raw_tile("wo_raw%d" % g)
-            load_dealt_rows(raw, wo[:, 512 * g : 512 * (g + 1)])
+            nc.sync.dma_start(raw[:], wo[:, 512 * g : 512 * (g + 1)].rearrange("(p i) c -> p i c", i=PACK))
             return raw
 
-        sb_win = zeroed_plane("sb_win", T)
+        sb_win = zeroed_plane("sb_win", T, "wa0_codes")
         sa_win = zeroed_plane("sa_win", T, "wa1_codes")
         w4s_raw = zeroed_plane("w4s_raw", PASSES * H).rearrange("p (a c) -> p a c", a=PASSES)
         sb_second = zeroed_plane("sb_second", S)
@@ -87,11 +83,12 @@ def tile_list_air_network_join_kernel(
         w8s_raw = zeroed_plane("w8s_raw", H)
 
         list_b = load_list("list_b", offs2)
-        tb0 = load_table_pass("tb0", tab2_words, 0, "sb")
-        load_packed_scales(sb_win, tab2_scales, nc.gpsimd)
-        tb1 = load_table_pass("tb1", tab2_words, 1, "wa0_codes")
+        tb0 = load_table_pass("tb0", tab2_words, 0, "window2")
+        tb1 = load_table_pass("tb1", tab2_words, 1, "window1")
+        load_packed_scales(sb_win, tab2_scales)
         list_a = load_list("list_a", offs)
         wa_raw0 = load_wa(0)
+        load_packed_scales(sa_win, tab_scales)
         wa_raw1 = load_wa(1)
         w4_raw = held.tile([P, PASSES, 2 * H], U8, name="w4_raw", align_bytes=64)
         nc.sync.dma_start(w4_raw[:].bitcast(I32), w4_words.rearrange("a p c -> p a c").bitcast(I32))
@@ -116,24 +113,8 @@ def tile_list_air_network_join_kernel(
                 )
             return got
 
-        def deal_words(name, raw, shape, dtype):
-            dealt = held.tile(shape, dtype, name=name, align_bytes=64)
-            src = raw.bitcast(I32)
-            dst = dealt[:].bitcast(I32)
-            if len(shape) == 3:
-                nc.vector.tensor_copy(
-                    dst.rearrange("p a (t b i) -> p a t b i", t=PACK, b=16),
-                    src.rearrange("p a (b t i) -> p a t b i", t=PACK, b=16),
-                )
-            else:
-                nc.vector.tensor_copy(
-                    dst.rearrange("p (t b i) -> p t b i", t=PACK, b=16),
-                    src.rearrange("p (b t i) -> p t b i", t=PACK, b=16),
-                )
-            return dealt
-
-        def rounded_tile(name):
-            return ring.tile([P, 512 * PACK], BF16, name=name, tag="rounded", bufs=2, align_bytes=64)
+        def rounded_tile(name, n):
+            return ring.tile([P, 512 * PACK], BF16, name=name, tag="rounded%d" % n, bufs=1, align_bytes=64)
 
         def quantize(name, rounded):
             codes = held.tile([P, 512], U32, name=name + "_codes", align_bytes=64)
@@ -142,15 +123,15 @@ def tile_list_air_network_join_kernel(
             return codes, scales
 
         def round_wa(a, raw):
-            rounded = rounded_tile("wa_bf%d" % a)
+            rounded = rounded_tile("wa_bf%d" % a, a)
             nc.scalar.copy(
-                rounded[:].rearrange("p (t b i j) -> p t b i j", t=PACK, i=RUN, j=PACK),
-                raw[:].rearrange("p j (b t i) -> p t b i j", t=PACK, i=RUN),
+                rounded[:].rearrange("p (c i j) -> p c j i", i=4, j=PACK),
+                raw[:].rearrange("p j (c i) -> p c j i", i=4),
             )
             return rounded
 
         def round_wo(g, raw):
-            rounded = rounded_tile("wo_bf%d" % g)
+            rounded = rounded_tile("wo_bf%d" % g, g)
             nc.scalar.copy(
                 rounded[:].rearrange("p (t m j) -> p m t j", t=PACK, j=PACK),
                 raw[:].rearrange("p j (m t) -> p m t j", t=PACK),
@@ -180,38 +161,38 @@ def tile_list_air_network_join_kernel(
         wa_bf0 = round_wa(0, wa_raw0)
         wa_bf1 = round_wa(1, wa_raw1)
         vb0 = gather_words("vb0", tb0, list_b, 1)
+        vb1 = gather_words("vb1", tb1, list_b, 1)
         sb = gather_scales("sb", sb_win, list_b)
-        load_packed_scales(sa_win, tab_scales)
-        nc.sync.dma_start(sb_second[0:112, :].bitcast(I32), sb[4:116, :].bitcast(I32))
         ta0 = load_table_pass("ta0", tab_words, 0, "window0")
+        nc.sync.dma_start(sb_second[0:112, :].bitcast(I32), sb[4:116, :].bitcast(I32))
         ta1 = load_table_pass("ta1", tab_words, 1, "window2")
         pick_b = load_list("pick_b", pos2)
         sp_sb = held.tile([P, PACK, J], F32, name="sp_sb", align_bytes=64)
-        load_dealt_rows(sp_sb, sp)
+        nc.sync.dma_start(sp_sb[:], sp.rearrange("(s p) j -> p s j", p=P))
         list_d = load_list("list_d", offs3)
         load_packed_scales(sd_win, tab3_scales)
-        w8_raw = held.tile([P, PASSES, H], I32, name="w8_raw", align_bytes=64)
-        nc.sync.dma_start(w8_raw[:], w8_words.rearrange("a p c i -> p a (c i)").bitcast(I32))
+        w8_raw = held.tile([P, PASSES, H], U32, name="w8_raw", align_bytes=64)
+        nc.sync.dma_start(w8_raw[:].bitcast(I32), w8_words.rearrange("a p c i -> p a (c i)").bitcast(I32))
         load_packed_scales(w8s_raw, w8_scales)
-        pick_a = load_list("pick_a", pos1)
         wo_raw0 = load_wo(0)
+        pick_a = load_list("pick_a", pos1)
         td0 = load_table_pass("td0", tab3_words, 0, "window0")
         wo_raw1 = load_wo(1)
         td1 = load_table_pass("td1", tab3_words, 1, "wo_codes")
         pick_d = load_list("pick_d", pos3)
 
-        vb1 = gather_words("vb1", tb1, list_b, HALVES)
-        w4 = deal_words("w4", w4_raw[:], [P, PASSES, 2 * H], U8)
-        w4s = deal_words("w4s", w4s_raw, [P, PASSES, H], U8)
         wa_q = [quantize("wa0", wa_bf0)]
         sa = gather_scales("sa", sa_win, list_a)
         wa_q.append(quantize("wa1", wa_bf1))
         b_rows = result_rows("b")
         first_stage(
             b_rows, range(HALVES),
-            lambda a, t: (w4[:, a, 2 * P * t : 2 * P * (t + 1)].bitcast(FP4X4), w4s[:, a, slice_cols(t)]),
+            lambda a, t: (w4_raw[:, a, 2 * P * t : 2 * P * (t + 1)].bitcast(FP4X4), w4s_raw[:, a, slice_cols(t)]),
             lambda a, cols: ((vb0, vb1)[a][:, cols].bitcast(FP8X4), (sb, sb_second)[a][:, cols]),
         )
+
+        ident = held.tile([P, P], F32, name="ident", align_bytes=64)
+        make_identity(nc, ident[:])
 
         va0 = gather_words("va0", ta0, list_a, 1)
         va1 = gather_words("va1", ta1, list_a, HALVES)
@@ -227,7 +208,7 @@ def tile_list_air_network_join_kernel(
         def d_half(h):
             first_stage(
                 d_rows, [h],
-                lambda a, t: (w8[:, a, slice_cols(t)].bitcast(FP8X4), w8s[4 * a : P, slice_cols(t)]),
+                lambda a, t: (w8_raw[:, a, slice_cols(t)].bitcast(FP8X4), w8s_raw[4 * a : P, slice_cols(t)]),
                 lambda a, cols: ((vd0, vd1)[a][:, cols].bitcast(FP8X4), sd[4 * a : P, cols]),
             )
 
@@ -246,7 +227,7 @@ def tile_list_air_network_join_kernel(
 
         def shortfall(c0, tag, bufs):
             below = ring.tile([P, PACK, CHUNK], F32, name="below", tag=tag, bufs=bufs, align_bytes=64)
-            short = ring.tile([P, PACK, CHUNK], F32, name="short", tag="short", bufs=1, align_bytes=64)
+            short = ring.tile([P, PACK, CHUNK], F32, name="short", tag="short", bufs=2, align_bytes=64)
             for t in range(PACK):
                 nc.vector.tensor_tensor(
                     below[:, t, :], b_rows[t][:].indirect(picks(pick_b, c0, CHUNK)), sp_sb[:, t, c0 : c0 + CHUNK], ALU.subtract
@@ -254,28 +235,42 @@ def tile_list_air_network_join_kernel(
             nc.scalar.activation(short[:], below[:], ACT.Relu, scale=-1.0)
             return short
 
-        def spread(c0, short, tag):
-            above = ring.tile([P, PACK, CHUNK], F32, name="above", tag=tag, bufs=1, align_bytes=64)
-            for t in range(PACK):
-                nc.vector.tensor_tensor(
-                    above[:, t, :], a_rows[t][:].indirect(picks(pick_a, c0, CHUNK)), sp_sb[:, t, c0 : c0 + CHUNK], ALU.subtract
-                )
-            nc.vector.scalar_tensor_tensor(above[:], above[:], 0.0, short[:], ALU.max, ALU.add)
-            return above
+        def excess(c0, tags):
+            over = ring.tile([P, PACK, CHUNK], F32, name="over", tag="over", bufs=2, align_bytes=64)
+            n = PACK // len(tags)
+            for part, tag in enumerate(tags):
+                above = ring.tile([P, n, CHUNK], F32, name="above", tag=tag, bufs=1, align_bytes=64)
+                for i in range(n):
+                    t = n * part + i
+                    nc.vector.tensor_tensor(
+                        above[:, i, :], a_rows[t][:].indirect(picks(pick_a, c0, CHUNK)), sp_sb[:, t, c0 : c0 + CHUNK], ALU.subtract
+                    )
+                nc.scalar.activation(over[:, n * part : n * (part + 1), :], above[:], ACT.Relu)
+            return over
 
-        def joined(j0, width, above, z_tag, tag):
-            inside = j0 % CHUNK
-            z = ring.tile([P, PACK, width], F32, name="z", tag=z_tag, bufs=1, align_bytes=64)
+        def surveys(j0, width, tag):
+            share = ring.tile([P, PACK, width], F32, name="share", tag=tag, bufs=1, align_bytes=64)
             for t in range(PACK):
-                nc.vector.tensor_tensor(
-                    z[:, t, :], d_rows[t][:].indirect(picks(pick_d, j0, width)),
-                    above[:, t, inside : inside + width], ALU.add,
+                nc.vector.tensor_copy(share[:, t, :], d_rows[t][:].indirect(picks(pick_d, j0, width)))
+            return share
+
+        def joined(addends, tag, words_out):
+            width = BLOCK
+            z_turned = psum.tile([P, PACK, P], F32, name="z_turned", tag="turn")
+            terms = [(t, x[:, t, :]) for x in addends for t in range(PACK)]
+            for n, (t, term) in enumerate(terms):
+                nc.tensor.matmul(
+                    z_turned[:, t, :], lhsT=term, rhs=ident[:], is_transpose=True,
+                    start=(n == 0), stop=(n == len(terms) - 1),
                 )
+            pairs = ring.tile([P, 2, P, 2], BF16, name="pairs", tag="pairs", bufs=2, align_bytes=64)
+            nc.scalar.copy(pairs[:], z_turned[:].rearrange("j s q -> j (s q)").rearrange("j (p u e) -> j u p e", u=2, e=2))
+            words = pairs[:].rearrange("j u p e -> j u (p e)").bitcast(F32)
+            z_back = psum.tile([P, 2, P], F32, name="z_back", tag="turn")
+            for u in range(2):
+                nc.tensor.transpose(z_back[:, u, :], words[:, u, :], ident[:])
             z_bf = ring.tile([P, width * PACK], BF16, name="z_bf", tag=tag, bufs=1, align_bytes=64)
-            nc.scalar.copy(
-                z_bf[:].rearrange("p (c i t) -> p c t i", i=4, t=PACK),
-                z[:].rearrange("p t (c i) -> p c t i", i=4),
-            )
+            words_out(z_bf[:].bitcast(F32).rearrange("p (j u) -> p j u", u=2), z_back[:].rearrange("p u j -> p j u"))
             z_codes = ring.tile([P, width], U32, name="z_codes", tag="z_codes", bufs=4, align_bytes=64)
             z_scales = ring.tile([P, width], U8, name="z_scales", tag="z_scales", bufs=4, align_bytes=64)
             nc.vector.quantize_mx(out=z_codes[:].bitcast(FP8X4), scales=z_scales[:], in_=z_bf[:])
@@ -288,7 +283,7 @@ def tile_list_air_network_join_kernel(
                 y_bf = ring.tile([P, width, PACK], BF16, name="y_bf", tag="y_bf", bufs=4, align_bytes=64)
                 for k in range(width // BLOCK):
                     block = slice(BLOCK * k, BLOCK * (k + 1))
-                    acc = psum.tile([P, PACK, BLOCK], F32, name="y_acc", tag="y_bank")
+                    acc = psum.tile([P, PACK, BLOCK], F32, name="y_acc", tag="bank")
                     for t in range(PACK):
                         nc.tensor.matmul_mx(
                             out=acc[:, t, :], lhsT=wo_codes[:, g, slice_cols(t)].bitcast(FP8X4),
@@ -315,9 +310,7 @@ def tile_list_air_network_join_kernel(
 
         short = shortfall(0, "below0", 1)
         sd = gather_scales("sd", sd_win, list_d)
-        w8 = deal_words("w8", w8_raw[:], [P, PASSES, H], U32)
-        w8s = deal_words("w8s", w8s_raw, [P, H], U8)
-        above = spread(0, short, "above0")
+        over = excess(0, ["above0"])
         wo_bf = [round_wo(0, wo_raw0), round_wo(1, wo_raw1)]
         vd0 = gather_words("vd0", td0, list_d, 1)
         vd1 = gather_words("vd1", td1, list_d, HALVES)
@@ -326,15 +319,27 @@ def tile_list_air_network_join_kernel(
         wo_codes = held.tile([P, GROUPS, 512], U32, name="wo_codes", align_bytes=64)
         quantize_wo(0, wo_bf[0])
         quantize_wo(1, wo_bf[1])
-        short = shortfall(CHUNK, "rounded", 2)
-        z_q = [joined(0, BLOCK, above, "z0", "above1"), joined(BLOCK, BLOCK, above, "z1", "z_bf1")]
+        short_next = shortfall(CHUNK, "rounded0", 1)
+        share = surveys(0, CHUNK, "share0")
+        halves = [slice(0, BLOCK), slice(BLOCK, CHUNK)]
+        over_next = excess(CHUNK, ["rounded0"])
+        z_q = [
+            joined([x[:, :, cols] for x in (short, over, share)], tag, nc.vector.tensor_copy)
+            for cols, tag in zip(halves, ("z_bf0", "z_bf1"))
+        ]
+
+        def late(k):
+            cols = halves[k]
+            share = surveys(CHUNK + cols.start, BLOCK, "z_bf%d" % k)
+            return joined([short_next[:, :, cols], over_next[:, :, cols], share[:]], "z_bf%d" % (k + 2), nc.vector.tensor_copy)
+
         second_stage(0, BLOCK, z_q[0], False)
-        second_stage(BLOCK, BLOCK, z_q[1], False)
+        z_q.append(late(0))
+        second_stage(BLOCK, BLOCK, z_q[1], True)
+        z_q.append(late(1))
         store_words(0)
-        above = spread(CHUNK, short, "above1")
-        z_q = [joined(CHUNK, BLOCK, above, "z0", "z_bf2"), joined(CHUNK + BLOCK, BLOCK, above, "z1", "z_bf1")]
-        second_stage(CHUNK, BLOCK, z_q[0], True)
-        second_stage(CHUNK + BLOCK, BLOCK, z_q[1], True)
+        second_stage(CHUNK, BLOCK, z_q[2], True)
+        second_stage(CHUNK + BLOCK, BLOCK, z_q[3], True)
         store_words(CHUNK)
 
         for q in range(QUADS):

@@ -19,14 +19,18 @@ ACT = mybir.ActivationFunctionType
 
 P = 128
 PACK = 4
-PASSES = K // (P * PACK)
-QUADS = 4
+K_PASS = P * PACK
+PASSES = K // K_PASS
+SLICES = H // P
+GROUPS = N // K_PASS
+QUADS, QUAD, SCALE_ROWS = 4, 32, 4
+STRIPE = 16
+LINE = 4
 BANK = 512
 HALVES = S // BANK
-GROUPS = N // (P * PACK)
-RUN = 8
-CHUNK = 256
-BLOCK = 128
+CHUNK = J // 2
+BLOCK = P
+EARLY = 2
 
 
 def tile_list_air_network_join_kernel(
@@ -37,313 +41,302 @@ def tile_list_air_network_join_kernel(
     nc = tc.nc
     with ExitStack() as ctx:
         held = ctx.enter_context(tc.tile_pool(name="held", bufs=1))
-        ring = ctx.enter_context(tc.tile_pool(name="ring", bufs=1))
+        work = ctx.enter_context(tc.tile_pool(name="work", bufs=1))
         psum = ctx.enter_context(tc.psum_pool(name="psum", bufs=4))
 
         def load_list(name, src):
-            lst = held.tile(list(src.shape), U16, name=name)
-            nc.sync.dma_start(lst[:], src)
-            return lst
+            entries = held.tile(list(src.shape), U16, name=name)
+            nc.sync.dma_start(entries[:], src)
+            return entries
 
-        def zeroed_plane(name, width, tag=None):
-            plane = held.tile([P, width], U8, name=name, tag=tag or name, align_bytes=64)
+        def zeroed_plane(name, width, tag):
+            plane = held.tile([P, width], U8, name=name, tag=tag, align_bytes=64)
             nc.vector.memset(plane[:].bitcast(I32), 0)
             return plane[:]
 
-        def load_packed_scales(plane, src):
+        def load_shared_plane(plane, scales):
             for q in range(QUADS):
                 nc.sync.dma_start(
-                    plane[32 * q : 32 * q + 4 * PASSES, :].bitcast(I32),
-                    src[:, 4 * q : 4 * q + 4, :].bitcast(I32),
+                    plane[QUAD * q : QUAD * q + SCALE_ROWS * PASSES, :].bitcast(I32),
+                    scales[:, SCALE_ROWS * q : SCALE_ROWS * (q + 1), :].bitcast(I32),
                 )
 
-        def load_table_pass(name, words, a, tag):
-            win = held.tile([P, T], I32, name=name, tag=tag, align_bytes=64)
-            nc.sync.dma_start(win[:], words[a].rearrange("p c i -> p (c i)").bitcast(I32))
-            return win
+        def load_table_pass(name, words, g, tag):
+            window = held.tile([P, T], I32, name=name, tag=tag, align_bytes=64)
+            nc.sync.dma_start(window[:], words[g].rearrange("p c t -> p (c t)").bitcast(I32))
+            return window
 
-        def raw_tile(name):
-            return ring.tile([P, PACK, 512], F32, name=name, tag="raw", bufs=2, align_bytes=64)
-
-        def load_wa(a):
-            raw = raw_tile("wa_raw%d" % a)
-            nc.sync.dma_start(raw[:], wa[512 * a : 512 * (a + 1), :].rearrange("(p i) c -> p i c", i=PACK))
+        def load_rows(name, rows, tag):
+            raw = work.tile([P, PACK, K_PASS], F32, name=name, tag=tag, align_bytes=64)
+            nc.sync.dma_start(raw[:], rows.rearrange("(p t) c -> p t c", t=PACK))
             return raw
 
-        def load_wo(g, tag=None):
-            raw = held.tile([P, PACK, 512], F32, name="wo_raw", tag=tag, align_bytes=64) if tag else raw_tile("wo_raw%d" % g)
-            nc.sync.dma_start(raw[:], wo[:, 512 * g : 512 * (g + 1)].rearrange("(p i) c -> p i c", i=PACK))
-            return raw
+        def gather_scales(name, plane, entries):
+            picked = held.tile([P, S], U8, name=name, align_bytes=64)
+            nc.vector.tensor_copy(picked[:], plane.indirect(entries[:]))
+            return picked
 
-        sb_win = zeroed_plane("sb_win", T, "wa0_codes")
-        sa_win = zeroed_plane("sa_win", T, "wa1_codes")
-        w4s_raw = zeroed_plane("w4s_raw", PASSES * H).rearrange("p (a c) -> p a c", a=PASSES)
-        sb_second = zeroed_plane("sb_second", S)
-        sd_win = zeroed_plane("sd_win", T)
-        w8s_raw = zeroed_plane("w8s_raw", H)
-
-        list_b = load_list("list_b", offs2)
-        tb0 = load_table_pass("tb0", tab2_words, 0, "window2")
-        tb1 = load_table_pass("tb1", tab2_words, 1, "window1")
-        load_packed_scales(sb_win, tab2_scales)
-        list_a = load_list("list_a", offs)
-        wa_raw0 = load_wa(0)
-        load_packed_scales(sa_win, tab_scales)
-        wa_raw1 = load_wa(1)
-        w4_raw = held.tile([P, PASSES, 2 * H], U8, name="w4_raw", align_bytes=64)
-        nc.sync.dma_start(w4_raw[:].bitcast(I32), w4_words.rearrange("a p c -> p a c").bitcast(I32))
-        for q in range(QUADS):
-            nc.sync.dma_start(
-                w4s_raw[32 * q : 32 * q + 4, :, :].bitcast(I32),
-                w4_scales[:, 4 * q : 4 * q + 4, :].rearrange("a r c -> r a c").bitcast(I32),
-            )
-
-        def gather_scales(name, win, lst):
-            got = held.tile([P, S], U8, name=name, align_bytes=64)
-            nc.vector.tensor_copy(got[:], win.indirect(lst[:]))
-            return got
-
-        def gather_words(name, win, lst, pieces):
-            got = held.tile([P, S], U32, name=name, align_bytes=64)
-            n = S // pieces
+        def gather_words(name, window, entries, pieces):
+            picked = held.tile([P, S], U32, name=name, align_bytes=64)
+            count = S // pieces
             for h in range(pieces):
                 nc.vector.tensor_copy(
-                    got[:, n * h : n * (h + 1)],
-                    win[:].bitcast(U32).indirect(lst[:, n // 16 * h : n // 16 * (h + 1)]),
+                    picked[:, count * h : count * (h + 1)],
+                    window[:].bitcast(U32).indirect(part_of(entries, count * h, count)),
                 )
-            return got
+            return picked
 
-        def rounded_tile(name, n):
-            return ring.tile([P, 512 * PACK], BF16, name=name, tag="rounded%d" % n, bufs=1, align_bytes=64)
+        def part_of(entries, start, count):
+            return entries[:, start // STRIPE : (start + count) // STRIPE]
 
-        def quantize(name, rounded):
-            codes = held.tile([P, 512], U32, name=name + "_codes", align_bytes=64)
-            scales = held.tile([P, 512], U8, name=name + "_scales", align_bytes=64)
-            nc.vector.quantize_mx(out=codes[:].bitcast(FP8X4), scales=scales[:], in_=rounded[:])
+        def round_wa(raw, tag):
+            rounded = work.tile([P, H * PACK], BF16, name="wa_rounded", tag=tag, align_bytes=64)
+            nc.scalar.copy(
+                rounded[:].rearrange("p (c i t) -> p c t i", i=LINE, t=PACK),
+                raw[:].rearrange("p t (c i) -> p c t i", i=LINE),
+            )
+            return rounded
+
+        def round_wo(raw, tag):
+            rounded = work.tile([P, K_PASS * PACK], BF16, name="wo_rounded", tag=tag, align_bytes=64)
+            nc.scalar.copy(
+                rounded[:].rearrange("p (f m t) -> p m f t", f=PACK, t=PACK),
+                raw[:].rearrange("p t (m f) -> p m f t", f=PACK),
+            )
+            return rounded
+
+        def quantize(codes, scales, rounded):
+            nc.vector.quantize_mx(out=codes.bitcast(FP8X4), scales=scales, in_=rounded)
+
+        def tile_cols(index):
+            return slice(P * index, P * (index + 1))
+
+        def first_stage(name, weights, columns):
+            rows = [held.tile([P, S], F32, name="%s_rows%d" % (name, s), align_bytes=64) for s in range(SLICES)]
+            for h in range(HALVES):
+                cols = slice(BANK * h, BANK * (h + 1))
+                for s in range(SLICES):
+                    acc = psum.tile([P, BANK], F32, name="acc", tag="sums")
+                    for g in range(PASSES):
+                        w_codes, w_scales = weights(g, s)
+                        v_codes, v_scales = columns(g, cols)
+                        nc.tensor.matmul_mx(
+                            out=acc[:], lhsT=w_codes, lhsT_scale=w_scales, rhs=v_codes, rhs_scale=v_scales,
+                            start=(g == 0), stop=(g == PASSES - 1),
+                        )
+                    nc.scalar.activation(rows[s][:, cols], acc[:], ACT.Copy)
+            return rows
+
+        def relu_of_gap(out, rows, entries, chunk, slices, sign, pool, tag):
+            gap = pool.tile([P, len(slices), CHUNK], F32, name="gap", tag=tag, align_bytes=64)
+            for s in slices:
+                nc.vector.tensor_tensor(
+                    gap[:, s - slices.start, :], rows[s][:].indirect(part_of(entries, CHUNK * chunk, CHUNK)),
+                    set_point[chunk][:, s, :], ALU.subtract,
+                )
+            nc.scalar.activation(out[:, slices.start : slices.stop, :], gap[:], ACT.Relu, scale=sign)
+
+        def chunk_tile(name, tag):
+            return work.tile([P, SLICES, CHUNK], F32, name=name, tag=tag, align_bytes=64)
+
+        def pick_surveys(j0, width, tag):
+            share = work.tile([P, SLICES, width], F32, name="share", tag=tag, align_bytes=64)
+            for s in range(SLICES):
+                nc.vector.tensor_copy(share[:, s, :], d_rows[s][:].indirect(part_of(pick_d, j0, width)))
+            return share
+
+        def turned_bank():
+            return psum.tile([P, SLICES, P], F32, name="z_turned", tag="turned", bufs=2)
+
+        def add_turned(z_turned, addend, first=False, last=False):
+            for s in range(SLICES):
+                nc.tensor.matmul(
+                    z_turned[:, s, :], lhsT=addend[:, s, :], rhs=identity[:], is_transpose=True,
+                    start=(first and s == 0), stop=(last and s == SLICES - 1),
+                )
+
+        def quantized_z(z_turned, pairs_tag, rounded_tag, copy_words):
+            pairs = work.tile([P, 2, P, 2], BF16, name="pairs", tag=pairs_tag, align_bytes=64)
+            nc.scalar.copy(
+                pairs[:], z_turned[:].rearrange("j s r -> j (s r)").rearrange("j (p u e) -> j u p e", u=2, e=2)
+            )
+            words = pairs[:].rearrange("j u p e -> j u (p e)").bitcast(F32)
+            z_back = psum.tile([P, 2, BLOCK], F32, name="z_back", tag="back", bufs=2)
+            for u in range(2):
+                nc.tensor.transpose(z_back[:, u, :], words[:, u, :], identity[:])
+            rounded = work.tile([P, BLOCK * PACK], BF16, name="z_rounded", tag=rounded_tag, align_bytes=64)
+            copy_words(rounded[:].bitcast(F32).rearrange("p (j u) -> p j u", u=2), z_back[:].rearrange("p u j -> p j u"))
+            codes = work.tile([P, BLOCK], U32, name="z_codes", bufs=J // BLOCK, align_bytes=64)
+            scales = work.tile([P, BLOCK], U8, name="z_scales", bufs=J // BLOCK, align_bytes=64)
+            quantize(codes[:], scales[:], rounded[:])
             return codes, scales
 
-        def round_wa(a, raw):
-            rounded = rounded_tile("wa_bf%d" % a, a)
-            nc.scalar.copy(
-                rounded[:].rearrange("p (c i j) -> p c j i", i=4, j=PACK),
-                raw[:].rearrange("p j (c i) -> p c j i", i=4),
-            )
-            return rounded
-
-        def round_wo(g, raw):
-            rounded = rounded_tile("wo_bf%d" % g, g)
-            nc.scalar.copy(
-                rounded[:].rearrange("p (t m j) -> p m t j", t=PACK, j=PACK),
-                raw[:].rearrange("p j (m t) -> p m t j", t=PACK),
-            )
-            return rounded
-
-        def result_rows(name):
-            return [held.tile([P, S], F32, name="%s_rows%d" % (name, t), align_bytes=64) for t in range(PACK)]
-
-        def first_stage(rows, halves, weights, columns):
-            for h in halves:
-                cols = slice(BANK * h, BANK * (h + 1))
+        def last_product(j0, z_quantized):
+            z_codes, z_scales = z_quantized
+            made = []
+            for g in range(GROUPS):
+                y = work.tile([P, PACK, BLOCK], F32, name="y", bufs=2 * GROUPS, align_bytes=64)
+                acc = psum.tile([P, PACK, BLOCK], F32, name="y_acc", tag="sums")
                 for t in range(PACK):
-                    acc = psum.tile([P, BANK], F32, name="acc", tag="bank")
-                    for a in range(PASSES):
-                        w_codes, w_scales = weights(a, t)
-                        c_codes, c_scales = columns(a, cols)
-                        nc.tensor.matmul_mx(
-                            out=acc[:], lhsT=w_codes, lhsT_scale=w_scales, rhs=c_codes, rhs_scale=c_scales,
-                            start=(a == 0), stop=(a == PASSES - 1),
-                        )
-                    nc.scalar.activation(rows[t][:, cols], acc[:], ACT.Copy)
+                    nc.tensor.matmul_mx(
+                        out=acc[:, t, :], lhsT=wo_codes[:, g, tile_cols(t)].bitcast(FP8X4),
+                        lhsT_scale=wo_scales[:, g, tile_cols(t)], rhs=z_codes[:].bitcast(FP8X4),
+                        rhs_scale=z_scales[:], start=True, stop=True,
+                    )
+                nc.scalar.copy(y[:], acc[:])
+                nc.sync.dma_start(out_rows[g][:, :, j0 : j0 + BLOCK], y[:])
+                made.append((acc, y))
+            return made
 
-        def slice_cols(t):
-            return slice(P * t, P * (t + 1))
+        def round_on_vector(rounded, acc, y):
+            nc.vector.tensor_copy(
+                rounded.rearrange("p (c i) t -> p c t i", i=LINE), y[:].rearrange("p t (c i) -> p c t i", i=LINE)
+            )
 
-        wa_bf0 = round_wa(0, wa_raw0)
-        wa_bf1 = round_wa(1, wa_raw1)
-        vb0 = gather_words("vb0", tb0, list_b, 1)
-        vb1 = gather_words("vb1", tb1, list_b, 1)
-        sb = gather_scales("sb", sb_win, list_b)
-        ta0 = load_table_pass("ta0", tab_words, 0, "window0")
-        nc.sync.dma_start(sb_second[0:112, :].bitcast(I32), sb[4:116, :].bitcast(I32))
-        ta1 = load_table_pass("ta1", tab_words, 1, "window2")
+        def round_on_scalar(rounded, acc, y):
+            nc.scalar.copy(rounded, acc[:].rearrange("p t j -> p j t"))
+
+        def quantize_y(j0, made, round_y, tags):
+            cols = slice(j0, j0 + BLOCK)
+            for g, (acc, y) in enumerate(made):
+                rounded = work.tile([P, BLOCK, PACK], BF16, name="y_rounded", tag=tags[g], align_bytes=64)
+                round_y(rounded[:], acc, y)
+                quantize(y_codes[:, g, cols], y_scales[:, g, cols], rounded[:].rearrange("p j t -> p (j t)"))
+
+        def store_words(chunk):
+            cols = slice(CHUNK * chunk, CHUNK * (chunk + 1))
+            nc.sync.dma_start(out_words[:, :, cols], y_codes[:, :, cols].bitcast(I32))
+
+        plane_b = zeroed_plane("plane_b", T, "plane_b")
+        plane_a = zeroed_plane("plane_a", T, "wa_codes")
+        w4_plane = zeroed_plane("w4_plane", PASSES * H, "w4_plane").rearrange("p (g c) -> p g c", g=PASSES)
+        scales_b1 = zeroed_plane("scales_b1", S, "scales_b1")
+        plane_d = zeroed_plane("plane_d", T, "plane_d")
+        w8_plane = zeroed_plane("w8_plane", H, "w8_plane")
+
+        list_b = load_list("list_b", offs2)
+        table_b0 = load_table_pass("table_b0", tab2_words, 0, "window2")
+        table_b1 = load_table_pass("table_b1", tab2_words, 1, "window1")
+        load_shared_plane(plane_b, tab2_scales)
+        list_a = load_list("list_a", offs)
+        wa_raw0 = load_rows("wa_raw0", wa[0:K_PASS, :], "raw0")
+        load_shared_plane(plane_a, tab_scales)
+        wa_raw1 = load_rows("wa_raw1", wa[K_PASS:K, :], "raw1")
+        w4 = held.tile([P, PASSES, 2 * H], U8, name="w4", align_bytes=64)
+        nc.sync.dma_start(w4[:].bitcast(I32), w4_words.rearrange("g p c -> p g c").bitcast(I32))
+        for q in range(QUADS):
+            nc.sync.dma_start(
+                w4_plane[QUAD * q : QUAD * q + SCALE_ROWS, :, :].bitcast(I32),
+                w4_scales[:, SCALE_ROWS * q : SCALE_ROWS * (q + 1), :].rearrange("g row c -> row g c").bitcast(I32),
+            )
+
+        wa_rounded = [round_wa(wa_raw0, "rounded0"), round_wa(wa_raw1, "rounded1")]
+        words_b = [gather_words("words_b0", table_b0, list_b, 1), gather_words("words_b1", table_b1, list_b, 1)]
+        scales_b = gather_scales("scales_b", plane_b, list_b)
+        table_a0 = load_table_pass("table_a0", tab_words, 0, "window0")
+        span = QUAD * (QUADS - 1) + SCALE_ROWS
+        nc.sync.dma_start(scales_b1[0:span, :].bitcast(I32), scales_b[SCALE_ROWS : SCALE_ROWS + span, :].bitcast(I32))
+        table_a1 = load_table_pass("table_a1", tab_words, 1, "window2")
         pick_b = load_list("pick_b", pos2)
-        sp_sb = held.tile([P, PACK, J], F32, name="sp_sb", align_bytes=64)
-        nc.sync.dma_start(sp_sb[:], sp.rearrange("(s p) j -> p s j", p=P))
+        set_point = [held.tile([P, SLICES, CHUNK], F32, name="set_point%d" % c, align_bytes=64) for c in range(J // CHUNK)]
+        sp_rows = sp.rearrange("(s p) j -> p s j", p=P)
+        nc.sync.dma_start(set_point[0][:], sp_rows[:, :, 0:CHUNK])
         list_d = load_list("list_d", offs3)
-        load_packed_scales(sd_win, tab3_scales)
-        w8_raw = held.tile([P, PASSES, H], U32, name="w8_raw", align_bytes=64)
-        nc.sync.dma_start(w8_raw[:].bitcast(I32), w8_words.rearrange("a p c i -> p a (c i)").bitcast(I32))
-        load_packed_scales(w8s_raw, w8_scales)
-        wo_raw0 = load_wo(0)
+        load_shared_plane(plane_d, tab3_scales)
+        w8 = held.tile([P, PASSES, H], U32, name="w8", align_bytes=64)
+        nc.sync.dma_start(w8[:].bitcast(I32), w8_words.rearrange("g p c t -> p g (c t)").bitcast(I32))
+        load_shared_plane(w8_plane, w8_scales)
         pick_a = load_list("pick_a", pos1)
-        td0 = load_table_pass("td0", tab3_words, 0, "window0")
-        wo_raw1 = load_wo(1)
-        td1 = load_table_pass("td1", tab3_words, 1, "wo_codes")
+        wo_raw0 = load_rows("wo_raw0", wo[:, 0:K_PASS], "raw0")
+        table_d0 = load_table_pass("table_d0", tab3_words, 0, "window1")
+        nc.sync.dma_start(set_point[1][:], sp_rows[:, :, CHUNK:J])
+        wo_raw1 = load_rows("wo_raw1", wo[:, K_PASS:N], "raw1")
+        table_d1 = load_table_pass("table_d1", tab3_words, 1, "wo_codes")
         pick_d = load_list("pick_d", pos3)
 
-        wa_q = [quantize("wa0", wa_bf0)]
-        sa = gather_scales("sa", sa_win, list_a)
-        wa_q.append(quantize("wa1", wa_bf1))
-        b_rows = result_rows("b")
-        first_stage(
-            b_rows, range(HALVES),
-            lambda a, t: (w4_raw[:, a, 2 * P * t : 2 * P * (t + 1)].bitcast(FP4X4), w4s_raw[:, a, slice_cols(t)]),
-            lambda a, cols: ((vb0, vb1)[a][:, cols].bitcast(FP8X4), (sb, sb_second)[a][:, cols]),
+        scales_a = gather_scales("scales_a", plane_a, list_a)
+        wa_codes = held.tile([P, PASSES, H], U32, name="wa_codes", align_bytes=64)
+        wa_scales = held.tile([P, PASSES, H], U8, name="wa_scales", align_bytes=64)
+        for g in range(PASSES):
+            quantize(wa_codes[:, g, :], wa_scales[:, g, :], wa_rounded[g][:])
+        b_rows = first_stage(
+            "b",
+            lambda g, s: (w4[:, g, 2 * P * s : 2 * P * (s + 1)].bitcast(FP4X4), w4_plane[:, g, tile_cols(s)]),
+            lambda g, cols: (words_b[g][:, cols].bitcast(FP8X4), (scales_b, scales_b1)[g][:, cols]),
         )
 
-        ident = held.tile([P, P], F32, name="ident", align_bytes=64)
-        make_identity(nc, ident[:])
+        identity = held.tile([P, P], F32, name="identity", align_bytes=64)
+        make_identity(nc, identity[:])
 
-        va0 = gather_words("va0", ta0, list_a, 1)
-        va1 = gather_words("va1", ta1, list_a, HALVES)
-        a_rows = result_rows("a")
-        first_stage(
-            a_rows, range(HALVES),
-            lambda a, t: (wa_q[a][0][:, slice_cols(t)].bitcast(FP8X4), wa_q[a][1][:, slice_cols(t)]),
-            lambda a, cols: ((va0, va1)[a][:, cols].bitcast(FP8X4), sa[4 * a : P, cols]),
+        words_a = [gather_words("words_a0", table_a0, list_a, 1), gather_words("words_a1", table_a1, list_a, HALVES)]
+        a_rows = first_stage(
+            "a",
+            lambda g, s: (wa_codes[:, g, tile_cols(s)].bitcast(FP8X4), wa_scales[:, g, tile_cols(s)]),
+            lambda g, cols: (words_a[g][:, cols].bitcast(FP8X4), scales_a[SCALE_ROWS * g : P, cols]),
         )
 
-        d_rows = result_rows("d")
+        every = range(SLICES)
+        short = [chunk_tile("short0", "short0")]
+        relu_of_gap(short[0], b_rows, pick_b, 0, every, -1.0, work, "gap_b")
+        scales_d = gather_scales("scales_d", plane_d, list_d)
+        wo_rounded = [round_wo(wo_raw0, "rounded0")]
+        over = [chunk_tile("over0", "raw0")]
+        relu_of_gap(over[0], a_rows, pick_a, 0, every, 1.0, work, "gap_a")
+        wo_rounded.append(round_wo(wo_raw1, "rounded1"))
 
-        def d_half(h):
-            first_stage(
-                d_rows, [h],
-                lambda a, t: (w8_raw[:, a, slice_cols(t)].bitcast(FP8X4), w8s_raw[4 * a : P, slice_cols(t)]),
-                lambda a, cols: ((vd0, vd1)[a][:, cols].bitcast(FP8X4), sd[4 * a : P, cols]),
-            )
-
-        wo_scales = held.tile([P, GROUPS, 512], U8, name="wo_scales", align_bytes=64)
-
-        def quantize_wo(g, rounded):
-            nc.vector.quantize_mx(out=wo_codes[:, g, :].bitcast(FP8X4), scales=wo_scales[:, g, :], in_=rounded[:])
+        words_d = [gather_words("words_d0", table_d0, list_d, 1)]
+        short.append(chunk_tile("short1", "raw1"))
+        relu_of_gap(short[1], b_rows, pick_b, 1, range(EARLY), -1.0, held, "window1")
+        words_d.append(gather_words("words_d1", table_d1, list_d, HALVES))
+        d_rows = first_stage(
+            "d",
+            lambda g, s: (w8[:, g, tile_cols(s)].bitcast(FP8X4), w8_plane[SCALE_ROWS * g : P, tile_cols(s)]),
+            lambda g, cols: (words_d[g][:, cols].bitcast(FP8X4), scales_d[SCALE_ROWS * g : P, cols]),
+        )
+        wo_codes = held.tile([P, GROUPS, K_PASS], U32, name="wo_codes", align_bytes=64)
+        wo_scales = held.tile([P, GROUPS, K_PASS], U8, name="wo_scales", align_bytes=64)
+        for g in range(GROUPS):
+            quantize(wo_codes[:, g, :], wo_scales[:, g, :], wo_rounded[g][:])
+        relu_of_gap(short[1], b_rows, pick_b, 1, range(EARLY, SLICES), -1.0, work, "rounded0")
 
         y_codes = held.tile([P, GROUPS, J], U32, name="y_codes", align_bytes=64)
         y_scales = held.tile([P, GROUPS, J], U8, name="y_scales", align_bytes=64)
         out_rows = out_0.rearrange("(g p t) j -> g p t j", p=P, t=PACK)
-        out_words = out_1.rearrange("g p m t -> p g (m t)").bitcast(I32)
+        out_words = out_1.rearrange("g p j t -> p g (j t)").bitcast(I32)
 
-        def picks(lst, start, count):
-            return lst[:, start // 16 : (start + count) // 16]
+        blocks = [slice(0, BLOCK), slice(BLOCK, CHUNK)]
+        share = pick_surveys(0, CHUNK, "share")
+        z = []
+        for blk, cols in enumerate(blocks):
+            z_turned = turned_bank()
+            add_turned(z_turned, short[0][:, :, cols], first=True)
+            add_turned(z_turned, over[0][:, :, cols])
+            add_turned(z_turned, share[:, :, cols], last=True)
+            z.append(quantized_z(z_turned, "pairs%d" % blk, "z_rounded%d" % blk, nc.scalar.copy))
 
-        def shortfall(c0, tag, bufs):
-            below = ring.tile([P, PACK, CHUNK], F32, name="below", tag=tag, bufs=bufs, align_bytes=64)
-            short = ring.tile([P, PACK, CHUNK], F32, name="short", tag="short", bufs=2, align_bytes=64)
-            for t in range(PACK):
-                nc.vector.tensor_tensor(
-                    below[:, t, :], b_rows[t][:].indirect(picks(pick_b, c0, CHUNK)), sp_sb[:, t, c0 : c0 + CHUNK], ALU.subtract
-                )
-            nc.scalar.activation(short[:], below[:], ACT.Relu, scale=-1.0)
-            return short
+        over.append(chunk_tile("over1", "pairs0"))
+        relu_of_gap(over[1], a_rows, pick_a, 1, every, 1.0, work, "rounded0")
+        late = [turned_bank() for cols in blocks]
+        for z_turned, cols in zip(late, blocks):
+            add_turned(z_turned, short[1][:, :, cols], first=True)
+        made0 = last_product(0, z[0])
+        for z_turned, cols in zip(late, blocks):
+            add_turned(z_turned, over[1][:, :, cols])
+        made1 = last_product(BLOCK, z[1])
+        for blk, cols in enumerate(blocks):
+            add_turned(late[blk], pick_surveys(CHUNK + cols.start, BLOCK, "z_rounded%d" % blk)[:], last=True)
+        for blk, z_turned in enumerate(late):
+            z.append(quantized_z(z_turned, "pairs%d" % (blk + 1), "z_rounded%d" % (blk + 2), nc.vector.tensor_copy))
 
-        def excess(c0, tags):
-            over = ring.tile([P, PACK, CHUNK], F32, name="over", tag="over", bufs=2, align_bytes=64)
-            n = PACK // len(tags)
-            for part, tag in enumerate(tags):
-                above = ring.tile([P, n, CHUNK], F32, name="above", tag=tag, bufs=1, align_bytes=64)
-                for i in range(n):
-                    t = n * part + i
-                    nc.vector.tensor_tensor(
-                        above[:, i, :], a_rows[t][:].indirect(picks(pick_a, c0, CHUNK)), sp_sb[:, t, c0 : c0 + CHUNK], ALU.subtract
-                    )
-                nc.scalar.activation(over[:, n * part : n * (part + 1), :], above[:], ACT.Relu)
-            return over
-
-        def surveys(j0, width, tag):
-            share = ring.tile([P, PACK, width], F32, name="share", tag=tag, bufs=1, align_bytes=64)
-            for t in range(PACK):
-                nc.vector.tensor_copy(share[:, t, :], d_rows[t][:].indirect(picks(pick_d, j0, width)))
-            return share
-
-        def joined(addends, tag, words_out):
-            width = BLOCK
-            z_turned = psum.tile([P, PACK, P], F32, name="z_turned", tag="turn")
-            terms = [(t, x[:, t, :]) for x in addends for t in range(PACK)]
-            for n, (t, term) in enumerate(terms):
-                nc.tensor.matmul(
-                    z_turned[:, t, :], lhsT=term, rhs=ident[:], is_transpose=True,
-                    start=(n == 0), stop=(n == len(terms) - 1),
-                )
-            pairs = ring.tile([P, 2, P, 2], BF16, name="pairs", tag="pairs", bufs=2, align_bytes=64)
-            nc.scalar.copy(pairs[:], z_turned[:].rearrange("j s q -> j (s q)").rearrange("j (p u e) -> j u p e", u=2, e=2))
-            words = pairs[:].rearrange("j u p e -> j u (p e)").bitcast(F32)
-            z_back = psum.tile([P, 2, P], F32, name="z_back", tag="turn")
-            for u in range(2):
-                nc.tensor.transpose(z_back[:, u, :], words[:, u, :], ident[:])
-            z_bf = ring.tile([P, width * PACK], BF16, name="z_bf", tag=tag, bufs=1, align_bytes=64)
-            words_out(z_bf[:].bitcast(F32).rearrange("p (j u) -> p j u", u=2), z_back[:].rearrange("p u j -> p j u"))
-            z_codes = ring.tile([P, width], U32, name="z_codes", tag="z_codes", bufs=4, align_bytes=64)
-            z_scales = ring.tile([P, width], U8, name="z_scales", tag="z_scales", bufs=4, align_bytes=64)
-            nc.vector.quantize_mx(out=z_codes[:].bitcast(FP8X4), scales=z_scales[:], in_=z_bf[:])
-            return z_codes, z_scales
-
-        def second_stage(j0, width, z_q, round_on_vector):
-            cols = slice(j0, j0 + width)
-            for g in range(GROUPS):
-                y = ring.tile([P, PACK, width], F32, name="y", tag="y", bufs=4, align_bytes=64)
-                y_bf = ring.tile([P, width, PACK], BF16, name="y_bf", tag="y_bf", bufs=4, align_bytes=64)
-                for k in range(width // BLOCK):
-                    block = slice(BLOCK * k, BLOCK * (k + 1))
-                    acc = psum.tile([P, PACK, BLOCK], F32, name="y_acc", tag="bank")
-                    for t in range(PACK):
-                        nc.tensor.matmul_mx(
-                            out=acc[:, t, :], lhsT=wo_codes[:, g, slice_cols(t)].bitcast(FP8X4),
-                            lhsT_scale=wo_scales[:, g, slice_cols(t)], rhs=z_q[0][:, block].bitcast(FP8X4),
-                            rhs_scale=z_q[1][:, block], start=True, stop=True,
-                        )
-                    nc.scalar.copy(y[:, :, block], acc[:])
-                    if round_on_vector:
-                        nc.vector.tensor_copy(
-                            y_bf[:, block, :].rearrange("p (c i) t -> p c t i", i=4),
-                            y[:, :, block].rearrange("p t (c i) -> p c t i", i=4),
-                        )
-                    else:
-                        nc.scalar.copy(y_bf[:, block, :], acc[:].rearrange("p t j -> p j t"))
-                nc.sync.dma_start(out_rows[g][:, :, cols], y[:])
-                nc.vector.quantize_mx(
-                    out=y_codes[:, g, cols].bitcast(FP8X4), scales=y_scales[:, g, cols],
-                    in_=y_bf[:].rearrange("p j t -> p (j t)"),
-                )
-
-        def store_words(c0):
-            cols = slice(c0, c0 + CHUNK)
-            nc.sync.dma_start(out_words[:, :, cols], y_codes[:, :, cols].bitcast(I32))
-
-        short = shortfall(0, "below0", 1)
-        sd = gather_scales("sd", sd_win, list_d)
-        over = excess(0, ["above0"])
-        wo_bf = [round_wo(0, wo_raw0), round_wo(1, wo_raw1)]
-        vd0 = gather_words("vd0", td0, list_d, 1)
-        vd1 = gather_words("vd1", td1, list_d, HALVES)
-        d_half(0)
-        d_half(1)
-        wo_codes = held.tile([P, GROUPS, 512], U32, name="wo_codes", align_bytes=64)
-        quantize_wo(0, wo_bf[0])
-        quantize_wo(1, wo_bf[1])
-        short_next = shortfall(CHUNK, "rounded0", 1)
-        share = surveys(0, CHUNK, "share0")
-        halves = [slice(0, BLOCK), slice(BLOCK, CHUNK)]
-        over_next = excess(CHUNK, ["rounded0"])
-        z_q = [
-            joined([x[:, :, cols] for x in (short, over, share)], tag, nc.vector.tensor_copy)
-            for cols, tag in zip(halves, ("z_bf0", "z_bf1"))
-        ]
-
-        def late(k):
-            cols = halves[k]
-            share = surveys(CHUNK + cols.start, BLOCK, "z_bf%d" % k)
-            return joined([short_next[:, :, cols], over_next[:, :, cols], share[:]], "z_bf%d" % (k + 2), nc.vector.tensor_copy)
-
-        second_stage(0, BLOCK, z_q[0], False)
-        z_q.append(late(0))
-        second_stage(BLOCK, BLOCK, z_q[1], True)
-        z_q.append(late(1))
+        quantize_y(0, made0, round_on_vector, ("y_rounded0", "y_rounded1"))
+        quantize_y(BLOCK, made1, round_on_scalar, ("pairs1", "pairs2"))
         store_words(0)
-        second_stage(CHUNK, BLOCK, z_q[2], True)
-        second_stage(CHUNK + BLOCK, BLOCK, z_q[3], True)
-        store_words(CHUNK)
+        quantize_y(CHUNK, last_product(CHUNK, z[2]), round_on_vector, ("y_rounded0", "y_rounded1"))
+        quantize_y(CHUNK + BLOCK, last_product(CHUNK + BLOCK, z[3]), round_on_vector, ("y_rounded2", "y_rounded3"))
+        store_words(1)
 
         for q in range(QUADS):
             nc.scalar.dma_start(
-                out_2[:, 4 * q : 4 * q + 4, :].rearrange("g r m -> r g m").bitcast(I32),
-                y_scales[32 * q : 32 * q + 4, :, :].bitcast(I32),
+                out_2[:, SCALE_ROWS * q : SCALE_ROWS * (q + 1), :].rearrange("g row j -> row g j").bitcast(I32),
+                y_scales[QUAD * q : QUAD * q + SCALE_ROWS, :, :].bitcast(I32),
             )

from contextlib import ExitStack

import concourse.mybir as mybir
from concourse.masks import make_identity

K, T, S, J, H, N = 1024, 2048, 1024, 512, 512, 1024
FLOPS = 2 * (3 * K * H * S + H * N * J)

F32 = mybir.dt.float32
BF16 = mybir.dt.bfloat16
I32 = mybir.dt.int32
U32 = mybir.dt.uint32
U16 = mybir.dt.uint16
U8 = mybir.dt.uint8
FP8X4 = mybir.dt.float8_e4m3fn_x4
FP4X4 = mybir.dt.float4_e2m1fn_x4
ALU = mybir.AluOpType
ACT = mybir.ActivationFunctionType

P = 128
PACK = 4
K_PASS = P * PACK
PASSES = K // K_PASS
SLICES = H // P
GROUPS = N // K_PASS
QUADS, QUAD, SCALE_ROWS = 4, 32, 4
STRIPE = 16
LINE = 4
BANK = 512
HALVES = S // BANK
CHUNK = J // 2
BLOCK = P
EARLY = 2


def tile_list_air_network_join_kernel(
    tc, tab_words, tab_scales, tab2_words, tab2_scales, tab3_words, tab3_scales,
    offs, offs2, offs3, pos1, pos2, pos3, wa, w4_words, w4_scales, w8_words, w8_scales, sp, wo,
    out_0, out_1, out_2,
):
    nc = tc.nc
    with ExitStack() as ctx:
        held = ctx.enter_context(tc.tile_pool(name="held", bufs=1))
        work = ctx.enter_context(tc.tile_pool(name="work", bufs=1))
        psum = ctx.enter_context(tc.psum_pool(name="psum", bufs=4))

        def load_list(name, src):
            entries = held.tile(list(src.shape), U16, name=name)
            nc.sync.dma_start(entries[:], src)
            return entries

        def zeroed_plane(name, width, tag):
            plane = held.tile([P, width], U8, name=name, tag=tag, align_bytes=64)
            nc.vector.memset(plane[:].bitcast(I32), 0)
            return plane[:]

        def load_shared_plane(plane, scales):
            for q in range(QUADS):
                nc.sync.dma_start(
                    plane[QUAD * q : QUAD * q + SCALE_ROWS * PASSES, :].bitcast(I32),
                    scales[:, SCALE_ROWS * q : SCALE_ROWS * (q + 1), :].bitcast(I32),
                )

        def load_table_pass(name, words, g, tag):
            window = held.tile([P, T], I32, name=name, tag=tag, align_bytes=64)
            nc.sync.dma_start(window[:], words[g].rearrange("p c t -> p (c t)").bitcast(I32))
            return window

        def load_rows(name, rows, tag):
            raw = work.tile([P, PACK, K_PASS], F32, name=name, tag=tag, align_bytes=64)
            nc.sync.dma_start(raw[:], rows.rearrange("(p t) c -> p t c", t=PACK))
            return raw

        def gather_scales(name, plane, entries):
            picked = held.tile([P, S], U8, name=name, align_bytes=64)
            nc.vector.tensor_copy(picked[:], plane.indirect(entries[:]))
            return picked

        def gather_words(name, window, entries, pieces):
            picked = held.tile([P, S], U32, name=name, align_bytes=64)
            count = S // pieces
            for h in range(pieces):
                nc.vector.tensor_copy(
                    picked[:, count * h : count * (h + 1)],
                    window[:].bitcast(U32).indirect(part_of(entries, count * h, count)),
                )
            return picked

        def part_of(entries, start, count):
            return entries[:, start // STRIPE : (start + count) // STRIPE]

        def round_wa(raw, tag):
            rounded = work.tile([P, H * PACK], BF16, name="wa_rounded", tag=tag, align_bytes=64)
            nc.scalar.copy(
                rounded[:].rearrange("p (c i t) -> p c t i", i=LINE, t=PACK),
                raw[:].rearrange("p t (c i) -> p c t i", i=LINE),
            )
            return rounded

        def round_wo(raw, tag):
            rounded = work.tile([P, K_PASS * PACK], BF16, name="wo_rounded", tag=tag, align_bytes=64)
            nc.scalar.copy(
                rounded[:].rearrange("p (f m t) -> p m f t", f=PACK, t=PACK),
                raw[:].rearrange("p t (m f) -> p m f t", f=PACK),
            )
            return rounded

        def quantize(codes, scales, rounded):
            nc.vector.quantize_mx(out=codes.bitcast(FP8X4), scales=scales, in_=rounded)

        def tile_cols(index):
            return slice(P * index, P * (index + 1))

        def first_stage(name, weights, columns):
            rows = [held.tile([P, S], F32, name="%s_rows%d" % (name, s), align_bytes=64) for s in range(SLICES)]
            for h in range(HALVES):
                cols = slice(BANK * h, BANK * (h + 1))
                for s in range(SLICES):
                    acc = psum.tile([P, BANK], F32, name="acc", tag="sums")
                    for g in range(PASSES):
                        w_codes, w_scales = weights(g, s)
                        v_codes, v_scales = columns(g, cols)
                        nc.tensor.matmul_mx(
                            out=acc[:], lhsT=w_codes, lhsT_scale=w_scales, rhs=v_codes, rhs_scale=v_scales,
                            start=(g == 0), stop=(g == PASSES - 1),
                        )
                    nc.scalar.activation(rows[s][:, cols], acc[:], ACT.Copy)
            return rows

        def relu_of_gap(out, rows, entries, chunk, slices, sign, pool, tag):
            gap = pool.tile([P, len(slices), CHUNK], F32, name="gap", tag=tag, align_bytes=64)
            for s in slices:
                nc.vector.tensor_tensor(
                    gap[:, s - slices.start, :], rows[s][:].indirect(part_of(entries, CHUNK * chunk, CHUNK)),
                    set_point[chunk][:, s, :], ALU.subtract,
                )
            nc.scalar.activation(out[:, slices.start : slices.stop, :], gap[:], ACT.Relu, scale=sign)

        def chunk_tile(name, tag):
            return work.tile([P, SLICES, CHUNK], F32, name=name, tag=tag, align_bytes=64)

        def pick_surveys(j0, width, tag):
            share = work.tile([P, SLICES, width], F32, name="share", tag=tag, align_bytes=64)
            for s in range(SLICES):
                nc.vector.tensor_copy(share[:, s, :], d_rows[s][:].indirect(part_of(pick_d, j0, width)))
            return share

        def turned_bank():
            return psum.tile([P, SLICES, P], F32, name="z_turned", tag="turned", bufs=2)

        def add_turned(z_turned, addend, first=False, last=False):
            for s in range(SLICES):
                nc.tensor.matmul(
                    z_turned[:, s, :], lhsT=addend[:, s, :], rhs=identity[:], is_transpose=True,
                    start=(first and s == 0), stop=(last and s == SLICES - 1),
                )

        def quantized_z(z_turned, pairs_tag, rounded_tag, copy_words):
            pairs = work.tile([P, 2, P, 2], BF16, name="pairs", tag=pairs_tag, align_bytes=64)
            nc.scalar.copy(
                pairs[:], z_turned[:].rearrange("j s r -> j (s r)").rearrange("j (p u e) -> j u p e", u=2, e=2)
            )
            words = pairs[:].rearrange("j u p e -> j u (p e)").bitcast(F32)
            z_back = psum.tile([P, 2, BLOCK], F32, name="z_back", tag="back", bufs=2)
            for u in range(2):
                nc.tensor.transpose(z_back[:, u, :], words[:, u, :], identity[:])
            rounded = work.tile([P, BLOCK * PACK], BF16, name="z_rounded", tag=rounded_tag, align_bytes=64)
            copy_words(rounded[:].bitcast(F32).rearrange("p (j u) -> p j u", u=2), z_back[:].rearrange("p u j -> p j u"))
            codes = work.tile([P, BLOCK], U32, name="z_codes", bufs=J // BLOCK, align_bytes=64)
            scales = work.tile([P, BLOCK], U8, name="z_scales", bufs=J // BLOCK, align_bytes=64)
            quantize(codes[:], scales[:], rounded[:])
            return codes, scales

        def last_product(j0, z_quantized):
            z_codes, z_scales = z_quantized
            made = []
            for g in range(GROUPS):
                y = work.tile([P, PACK, BLOCK], F32, name="y", bufs=2 * GROUPS, align_bytes=64)
                acc = psum.tile([P, PACK, BLOCK], F32, name="y_acc", tag="sums")
                for t in range(PACK):
                    nc.tensor.matmul_mx(
                        out=acc[:, t, :], lhsT=wo_codes[:, g, tile_cols(t)].bitcast(FP8X4),
                        lhsT_scale=wo_scales[:, g, tile_cols(t)], rhs=z_codes[:].bitcast(FP8X4),
                        rhs_scale=z_scales[:], start=True, stop=True,
                    )
                nc.scalar.copy(y[:], acc[:])
                nc.sync.dma_start(out_rows[g][:, :, j0 : j0 + BLOCK], y[:])
                made.append((acc, y))
            return made

        def round_on_vector(rounded, acc, y):
            nc.vector.tensor_copy(
                rounded.rearrange("p (c i) t -> p c t i", i=LINE), y[:].rearrange("p t (c i) -> p c t i", i=LINE)
            )

        def round_on_scalar(rounded, acc, y):
            nc.scalar.copy(rounded, acc[:].rearrange("p t j -> p j t"))

        def quantize_y(j0, made, round_y, tags):
            cols = slice(j0, j0 + BLOCK)
            for g, (acc, y) in enumerate(made):
                rounded = work.tile([P, BLOCK, PACK], BF16, name="y_rounded", tag=tags[g], align_bytes=64)
                round_y(rounded[:], acc, y)
                quantize(y_codes[:, g, cols], y_scales[:, g, cols], rounded[:].rearrange("p j t -> p (j t)"))

        def store_words(chunk):
            cols = slice(CHUNK * chunk, CHUNK * (chunk + 1))
            nc.sync.dma_start(out_words[:, :, cols], y_codes[:, :, cols].bitcast(I32))

        plane_b = zeroed_plane("plane_b", T, "plane_b")
        plane_a = zeroed_plane("plane_a", T, "wa_codes")
        w4_plane = zeroed_plane("w4_plane", PASSES * H, "w4_plane").rearrange("p (g c) -> p g c", g=PASSES)
        scales_b1 = zeroed_plane("scales_b1", S, "scales_b1")
        plane_d = zeroed_plane("plane_d", T, "plane_d")
        w8_plane = zeroed_plane("w8_plane", H, "w8_plane")

        list_b = load_list("list_b", offs2)
        table_b0 = load_table_pass("table_b0", tab2_words, 0, "window2")
        table_b1 = load_table_pass("table_b1", tab2_words, 1, "window1")
        load_shared_plane(plane_b, tab2_scales)
        list_a = load_list("list_a", offs)
        wa_raw0 = load_rows("wa_raw0", wa[0:K_PASS, :], "raw0")
        load_shared_plane(plane_a, tab_scales)
        wa_raw1 = load_rows("wa_raw1", wa[K_PASS:K, :], "raw1")
        w4 = held.tile([P, PASSES, 2 * H], U8, name="w4", align_bytes=64)
        nc.sync.dma_start(w4[:].bitcast(I32), w4_words.rearrange("g p c -> p g c").bitcast(I32))
        for q in range(QUADS):
            nc.sync.dma_start(
                w4_plane[QUAD * q : QUAD * q + SCALE_ROWS, :, :].bitcast(I32),
                w4_scales[:, SCALE_ROWS * q : SCALE_ROWS * (q + 1), :].rearrange("g row c -> row g c").bitcast(I32),
            )

        wa_rounded = [round_wa(wa_raw0, "rounded0"), round_wa(wa_raw1, "rounded1")]
        words_b = [gather_words("words_b0", table_b0, list_b, 1), gather_words("words_b1", table_b1, list_b, 1)]
        scales_b = gather_scales("scales_b", plane_b, list_b)
        table_a0 = load_table_pass("table_a0", tab_words, 0, "window0")
        span = QUAD * (QUADS - 1) + SCALE_ROWS
        nc.sync.dma_start(scales_b1[0:span, :].bitcast(I32), scales_b[SCALE_ROWS : SCALE_ROWS + span, :].bitcast(I32))
        table_a1 = load_table_pass("table_a1", tab_words, 1, "window2")
        pick_b = load_list("pick_b", pos2)
        set_point = [held.tile([P, SLICES, CHUNK], F32, name="set_point%d" % c, align_bytes=64) for c in range(J // CHUNK)]
        sp_rows = sp.rearrange("(s p) j -> p s j", p=P)
        nc.sync.dma_start(set_point[0][:], sp_rows[:, :, 0:CHUNK])
        list_d = load_list("list_d", offs3)
        load_shared_plane(plane_d, tab3_scales)
        w8 = held.tile([P, PASSES, H], U32, name="w8", align_bytes=64)
        nc.sync.dma_start(w8[:].bitcast(I32), w8_words.rearrange("g p c t -> p g (c t)").bitcast(I32))
        load_shared_plane(w8_plane, w8_scales)
        pick_a = load_list("pick_a", pos1)
        wo_raw0 = load_rows("wo_raw0", wo[:, 0:K_PASS], "raw0")
        table_d0 = load_table_pass("table_d0", tab3_words, 0, "window1")
        nc.sync.dma_start(set_point[1][:], sp_rows[:, :, CHUNK:J])
        wo_raw1 = load_rows("wo_raw1", wo[:, K_PASS:N], "raw1")
        table_d1 = load_table_pass("table_d1", tab3_words, 1, "wo_codes")
        pick_d = load_list("pick_d", pos3)

        scales_a = gather_scales("scales_a", plane_a, list_a)
        wa_codes = held.tile([P, PASSES, H], U32, name="wa_codes", align_bytes=64)
        wa_scales = held.tile([P, PASSES, H], U8, name="wa_scales", align_bytes=64)
        for g in range(PASSES):
            quantize(wa_codes[:, g, :], wa_scales[:, g, :], wa_rounded[g][:])
        b_rows = first_stage(
            "b",
            lambda g, s: (w4[:, g, 2 * P * s : 2 * P * (s + 1)].bitcast(FP4X4), w4_plane[:, g, tile_cols(s)]),
            lambda g, cols: (words_b[g][:, cols].bitcast(FP8X4), (scales_b, scales_b1)[g][:, cols]),
        )

        identity = held.tile([P, P], F32, name="identity", align_bytes=64)
        make_identity(nc, identity[:])

        words_a = [gather_words("words_a0", table_a0, list_a, 1), gather_words("words_a1", table_a1, list_a, HALVES)]
        a_rows = first_stage(
            "a",
            lambda g, s: (wa_codes[:, g, tile_cols(s)].bitcast(FP8X4), wa_scales[:, g, tile_cols(s)]),
            lambda g, cols: (words_a[g][:, cols].bitcast(FP8X4), scales_a[SCALE_ROWS * g : P, cols]),
        )

        every = range(SLICES)
        short = [chunk_tile("short0", "short0")]
        relu_of_gap(short[0], b_rows, pick_b, 0, every, -1.0, work, "gap_b")
        scales_d = gather_scales("scales_d", plane_d, list_d)
        wo_rounded = [round_wo(wo_raw0, "rounded0")]
        over = [chunk_tile("over0", "raw0")]
        relu_of_gap(over[0], a_rows, pick_a, 0, every, 1.0, work, "gap_a")
        wo_rounded.append(round_wo(wo_raw1, "rounded1"))

        words_d = [gather_words("words_d0", table_d0, list_d, 1)]
        short.append(chunk_tile("short1", "raw1"))
        relu_of_gap(short[1], b_rows, pick_b, 1, range(EARLY), -1.0, held, "window1")
        words_d.append(gather_words("words_d1", table_d1, list_d, HALVES))
        d_rows = first_stage(
            "d",
            lambda g, s: (w8[:, g, tile_cols(s)].bitcast(FP8X4), w8_plane[SCALE_ROWS * g : P, tile_cols(s)]),
            lambda g, cols: (words_d[g][:, cols].bitcast(FP8X4), scales_d[SCALE_ROWS * g : P, cols]),
        )
        wo_codes = held.tile([P, GROUPS, K_PASS], U32, name="wo_codes", align_bytes=64)
        wo_scales = held.tile([P, GROUPS, K_PASS], U8, name="wo_scales", align_bytes=64)
        for g in range(GROUPS):
            quantize(wo_codes[:, g, :], wo_scales[:, g, :], wo_rounded[g][:])
        relu_of_gap(short[1], b_rows, pick_b, 1, range(EARLY, SLICES), -1.0, work, "rounded0")

        y_codes = held.tile([P, GROUPS, J], U32, name="y_codes", align_bytes=64)
        y_scales = held.tile([P, GROUPS, J], U8, name="y_scales", align_bytes=64)
        out_rows = out_0.rearrange("(g p t) j -> g p t j", p=P, t=PACK)
        out_words = out_1.rearrange("g p j t -> p g (j t)").bitcast(I32)

        blocks = [slice(0, BLOCK), slice(BLOCK, CHUNK)]
        share = pick_surveys(0, CHUNK, "share")
        z = []
        for blk, cols in enumerate(blocks):
            z_turned = turned_bank()
            add_turned(z_turned, short[0][:, :, cols], first=True)
            add_turned(z_turned, over[0][:, :, cols])
            add_turned(z_turned, share[:, :, cols], last=True)
            z.append(quantized_z(z_turned, "pairs%d" % blk, "z_rounded%d" % blk, nc.scalar.copy))

        over.append(chunk_tile("over1", "pairs0"))
        relu_of_gap(over[1], a_rows, pick_a, 1, every, 1.0, work, "rounded0")
        late = [turned_bank() for cols in blocks]
        for z_turned, cols in zip(late, blocks):
            add_turned(z_turned, short[1][:, :, cols], first=True)
        made0 = last_product(0, z[0])
        for z_turned, cols in zip(late, blocks):
            add_turned(z_turned, over[1][:, :, cols])
        made1 = last_product(BLOCK, z[1])
        for blk, cols in enumerate(blocks):
            add_turned(late[blk], pick_surveys(CHUNK + cols.start, BLOCK, "z_rounded%d" % blk)[:], last=True)
        for blk, z_turned in enumerate(late):
            z.append(quantized_z(z_turned, "pairs%d" % (blk + 1), "z_rounded%d" % (blk + 2), nc.vector.tensor_copy))

        quantize_y(0, made0, round_on_vector, ("y_rounded0", "y_rounded1"))
        quantize_y(BLOCK, made1, round_on_scalar, ("pairs1", "pairs2"))
        store_words(0)
        quantize_y(CHUNK, last_product(CHUNK, z[2]), round_on_vector, ("y_rounded0", "y_rounded1"))
        quantize_y(CHUNK + BLOCK, last_product(CHUNK + BLOCK, z[3]), round_on_vector, ("y_rounded2", "y_rounded3"))
        store_words(1)

        for q in range(QUADS):
            nc.scalar.dma_start(
                out_2[:, SCALE_ROWS * q : SCALE_ROWS * (q + 1), :].rearrange("g row j -> row g j").bitcast(I32),
                y_scales[QUAD * q : QUAD * q + SCALE_ROWS, :, :].bitcast(I32),
            )
